import numpy as np
import ml_dtypes


def mxq(x, axis, fmt="e4m3"):
    dtype, down = {"e4m3": (ml_dtypes.float8_e4m3fn, 7), "e5m2": (ml_dtypes.float8_e5m2, 14)}[fmt]
    v = np.moveaxis(np.asarray(x, np.float32).astype(ml_dtypes.bfloat16).astype(np.float64), axis, -1)
    blocks = v.reshape(v.shape[:-1] + (-1, 32))
    amax = np.abs(blocks).max(-1, keepdims=True)
    byte = np.maximum(np.where(amax > 0, np.frexp(amax)[1] - 1 + 127, 0) - down, 1)
    scale = np.exp2(byte - 127.0)
    codes = (blocks / scale).astype(np.float32).astype(dtype).astype(np.float64)
    return np.moveaxis((codes * scale).reshape(v.shape), -1, axis)


WIDE = False


def mx_kscale(k):
    if not WIDE:
        return np.ones(k)
    levels = np.array([10, -10, 5, -5, 0])
    if k % 512:
        return np.exp2(np.random.permutation(np.resize(levels, k // 32))).repeat(32)
    a = np.empty((k // 512, 16))
    for p in range(k // 512):
        a[p, :8] = np.random.permutation(np.resize(levels, 8))
        for g in range(8):
            far = levels[np.abs(levels - a[p, g]) >= 10]
            a[p, g + 8] = far[np.random.randint(len(far))]
    return np.exp2(a.ravel()).repeat(32)


BF16 = ml_dtypes.bfloat16


def bf(x):
    return np.asarray(x, np.float32).astype(BF16)


def f64(x):
    return np.asarray(x).astype(np.float64)


E2M1 = np.array([0.0, 0.5, 1.0, 1.5, 2.0, 3.0, 4.0, 6.0, -0.0, -0.5, -1.0, -1.5, -2.0, -3.0, -4.0, -6.0])


def pack_weight(w, fmt):
    k, n = w.shape
    w = f64(bf(w)).reshape(k // 32, 32, n)
    amax = np.abs(w).max(1)
    if fmt == "e4m3":
        byte = np.frexp(amax)[1] - 1 + 127 - 7
    else:
        mant, ex = np.frexp(amax / 6.0)
        byte = np.where(mant > 0.5, ex, ex - 1) + 127
    byte = np.clip(np.where(amax > 0, byte, 1), 1, 254)
    scaled = (w * np.exp2(127.0 - byte)[:, None, :]).reshape(k, n).astype(np.float32)
    by_word = np.ascontiguousarray(scaled.reshape(k // 512, 128, 4, n).transpose(0, 1, 3, 2))
    if fmt == "e4m3":
        words = by_word.astype(ml_dtypes.float8_e4m3fn).view(np.uint8)
    else:
        c = by_word.astype(ml_dtypes.float4_e2m1fn).view(np.uint8) & 0xF
        words = c[..., 0::2] | (c[..., 1::2] << 4)
    return np.ascontiguousarray(words), np.ascontiguousarray(byte.astype(np.uint8).reshape(k // 512, 16, n))


def unpack_weight(words, scales, fmt):
    g, p, n, _ = words.shape
    if fmt == "e4m3":
        vals = np.ascontiguousarray(words).view(ml_dtypes.float8_e4m3fn).astype(np.float64)
    else:
        nib = np.empty((g, p, n, 4), np.uint8)
        nib[..., 0::2] = words & 0xF
        nib[..., 1::2] = words >> 4
        vals = E2M1[nib]
    vals = vals * np.repeat(np.exp2(scales.astype(np.float64) - 127.0), 8, axis=1)[..., None]
    return vals.transpose(0, 1, 3, 2).reshape(g * 512, n)
def pack4(w):
    words, scales = pack_weight(w, "e2m1")
    return words.reshape(words.shape[0], 128, -1), scales


def unpack4(words, scales):
    return unpack_weight(words.reshape(words.shape[0], 128, -1, 2), scales, "e2m1")


def planes(Y):
    n, m = Y.shape
    b = f64(bf(Y)).reshape(n // 32, 32, m)
    amax = np.abs(b).max(1)
    byte = np.clip(np.where(amax > 0, np.frexp(amax)[1] - 1 + 127 - 7, 1), 1, 254)
    codes = (b * np.exp2(127.0 - byte)[:, None, :]).reshape(n, m).astype(np.float32).astype(ml_dtypes.float8_e4m3fn).view(np.uint8)
    words = codes.reshape(n // 512, 128, 4, m).transpose(0, 1, 3, 2)
    return np.ascontiguousarray(words), np.ascontiguousarray(byte.astype(np.uint8).reshape(n // 512, 16, m))


R, P, F = 1536, 512, 1024

REACH = 0.1

def standardise(v):
    return (v - v.mean(0)) / v.std(0)

def unit_weights(w):
    w = w * (1.0 - np.eye(R))
    return w / np.sqrt(np.square(w).sum(0))

def setup_inputs():
    s_far, s_near, t_lag = mx_kscale(R), mx_kscale(R), mx_kscale(P)
    px, py = np.random.rand(R), np.random.rand(R)
    dist = np.hypot(px[:, None] - px, py[:, None] - py)
    far = unit_weights(np.exp(-dist / REACH))
    near = unit_weights(np.exp(np.random.randn(R, R)))
    near_words, near_scales = pack4(near / s_near[:, None])
    z_prev = standardise(np.random.randn(R, P))
    z_now = standardise(np.random.randn(R, P))
    gain = 1 + 0.1 * np.random.randn(P)
    load = np.random.randn(P, F) / np.sqrt(P)
    x = standardise(np.random.randn(R, F))
    region_weight = np.exp(0.8 * np.random.randn(R))
    return {"far": bf(far / s_far[:, None]), "z_prev": bf(z_prev * s_far[:, None]),
            "near_words": near_words, "near_scales": near_scales, "z_now": bf(z_now * s_near[:, None]),
            "gain": bf(gain * t_lag), "load": bf(load / t_lag[:, None]),
            "x": bf(x), "region_weight": bf(region_weight)}

def reference(far, z_prev, near_words, near_scales, z_now, gain, load, x, region_weight):
    lag_far = mxq(f64(far), 0).T @ mxq(f64(z_prev), 0)
    lag_near = unpack4(near_words, near_scales).T @ mxq(f64(z_now), 0)
    lag = (lag_far + lag_near) * f64(gain)
    comp = mxq(lag, 1) @ mxq(f64(load), 0)
    y = comp * f64(x) * f64(region_weight)[:, None]
    Y = y.reshape(R, F)
    words, scales = planes(Y)
    return y, words, scales

@@ -1,0 +1,368 @@
+from contextlib import ExitStack
+
+import concourse.mybir as mybir
+
+R, C, F = 1536, 512, 1024
+P = 128
+PACK = 4
+SPAN = P * PACK
+GROUPS = R // SPAN
+HALVES = F // SPAN
+RAW_BUFS = 10
+GROUPED_BUFS = 6
+Y_BUFS = 6
+CODE_BUFS = {"zp": 3, "zn": 3, "far": 9, "load": 2, "lag": 3}
+LAG_SET = (0, 1, 1)
+Y_PAIR = (0, 1, 0, 1, 1, 2, 0, 3, 1, 3, 0, 0)
+FLOPS = 2 * (2 * R * R * C + R * C * F)
+
+F32 = mybir.dt.float32
+BF16 = mybir.dt.bfloat16
+I32 = mybir.dt.int32
+U32 = mybir.dt.uint32
+U8 = mybir.dt.uint8
+FP8X4 = mybir.dt.float8_e4m3fn_x4
+FP4X4 = mybir.dt.float4_e2m1fn_x4
+MULT = mybir.AluOpType.mult
+COPY = mybir.ActivationFunctionType.Copy
+
+
+def tile_local_bivariate_moran_k6_kernel(
+    tc, far, z_prev, near_words, near_scales, z_now, gain, load, x, region_weight, out_0, out_1, out_2
+):
+    nc = tc.nc
+    with ExitStack() as ctx:
+        keep = ctx.enter_context(tc.tile_pool(name="keep", bufs=1))
+        stream = ctx.enter_context(tc.tile_pool(name="stream", bufs=1))
+        psum = ctx.enter_context(tc.psum_pool(name="psum", bufs=1))
+        ctx.enter_context(tc.manual_schedule())
+
+        raw, grouped, codes, scales = {}, {}, {}, {}
+        near, xs, lag_bank, y_bank, ys, y_codes, y_scales = {}, {}, {}, {}, {}, {}, {}
+
+        def copier(engine):
+            return nc.vector.tensor_copy if engine == "V" else nc.scalar.copy
+
+        def load_rows(key, rows):
+            raw[key] = stream.tile([P, PACK, SPAN], BF16, name="raw", bufs=RAW_BUFS, align_bytes=64)
+            nc.sync.dma_start(out=raw[key][:], in_=rows.rearrange("(p j) w -> p j w", j=PACK))
+
+        def load_z(which, c):
+            src = z_prev if which == "zp" else z_now
+            load_rows((which, c), src[c * SPAN : (c + 1) * SPAN, :])
+
+        def load_far(c, g):
+            load_rows(("far", c, g), far[c * SPAN : (c + 1) * SPAN, g * SPAN : (g + 1) * SPAN])
+
+        def load_load():
+            whole = keep.tile([P, PACK, F], BF16, name="load_raw", align_bytes=64)
+            nc.sync.dma_start(out=whole[:], in_=load.rearrange("(p j) f -> p j f", j=PACK))
+            for h in range(HALVES):
+                raw[("load", h)] = whole[:, :, h * SPAN : (h + 1) * SPAN]
+
+        def load_near(g0, g1):
+            words = keep.tile([P, GROUPS, (g1 - g0) * 2 * SPAN], U8, name="near%d" % g0, align_bytes=64)
+            nc.sync.dma_start(
+                out=words[:].bitcast(I32),
+                in_=near_words.rearrange("c p n -> p c n")[:, :, g0 * 2 * SPAN : g1 * 2 * SPAN].bitcast(I32),
+            )
+            for g in range(g0, g1):
+                near[g] = words[:, :, (g - g0) * 2 * SPAN : (g - g0 + 1) * 2 * SPAN]
+
+        def load_near_scales():
+            for r in range(4):
+                nc.sync.dma_start(
+                    out=near_plane[r:P:32, :, :].bitcast(I32),
+                    in_=near_scales[:, r:16:4, :].rearrange("c q n -> q c n").bitcast(I32),
+                )
+
+        def load_x(g):
+            xs[g] = keep.tile([P, PACK, F], BF16, name="x%d" % g, align_bytes=64)
+            nc.sync.dma_start(
+                out=xs[g][:], in_=x[g * SPAN : (g + 1) * SPAN, :].rearrange("(p j) f -> p j f", j=PACK)
+            )
+
+        def grouped_tile(key):
+            if key not in grouped:
+                grouped[key] = stream.tile([P, SPAN, PACK], BF16, name="grouped", bufs=GROUPED_BUFS, align_bytes=64)
+            return grouped[key]
+
+        def weave(key, engine, lo, hi):
+            dst = grouped_tile(key)[:, lo:hi, :].rearrange("p (c i) j -> p c j i", i=4)
+            src = raw[key][:, :, lo:hi].rearrange("p j (c i) -> p c j i", i=4)
+            copier(engine)(out=dst, in_=src)
+
+        def weave_z(key, engine, t0, t1):
+            dst = grouped_tile(key)[:].rearrange("p (t a b) j -> p a t b j", t=PACK, b=2)[:, :, t0:t1, :, :]
+            src = raw[key][:].rearrange("p j (a b t) -> p a t b j", t=PACK, b=2)[:, :, t0:t1, :, :]
+            copier(engine)(out=dst, in_=src)
+
+        def quantize(key):
+            tag = key[0]
+            bufs = CODE_BUFS[tag]
+            codes[key] = stream.tile([P, SPAN], U32, name=tag + "_codes", bufs=bufs, align_bytes=64)
+            scales[key] = stream.tile([P, SPAN], U8, name=tag + "_scales", bufs=bufs, align_bytes=64)
+            nc.vector.quantize_mx(
+                out=codes[key][:].bitcast(FP8X4),
+                scales=scales[key][:],
+                in_=grouped[key][:].rearrange("p w j -> p (w j)"),
+            )
+
+        def lag_pass(g, which, c, first, last):
+            for t in range(PACK):
+                if first:
+                    lag_bank[(g, t)] = psum.tile([P, SPAN], F32, name="bank%d" % (PACK * LAG_SET[g] + t))
+                cols = slice(t * P, (t + 1) * P)
+                if which == "zp":
+                    rhs, rhs_scale = codes[("far", c, g)][:].bitcast(FP8X4), scales[("far", c, g)][:]
+                else:
+                    rhs, rhs_scale = near[g][:, c, :].bitcast(FP4X4), near_plane[:, c, g * SPAN : (g + 1) * SPAN]
+                nc.tensor.matmul_mx(
+                    out=lag_bank[(g, t)][:],
+                    lhsT=codes[(which, c)][:, cols].bitcast(FP8X4),
+                    lhsT_scale=scales[(which, c)][:, cols],
+                    rhs=rhs,
+                    rhs_scale=rhs_scale,
+                    start=first,
+                    stop=last,
+                )
+
+        def lag_out(g, t0=0, t1=PACK):
+            if t0 == 0:
+                raw[("lag", g)] = stream.tile([P, PACK, SPAN], BF16, name="lag_raw", bufs=2, align_bytes=64)
+            for t in range(t0, t1):
+                nc.scalar.activation(
+                    out=raw[("lag", g)][:, t, :].rearrange("p (s m) -> p s m", s=PACK),
+                    in_=lag_bank[(g, t)][:].rearrange("p (m s) -> p s m", s=PACK),
+                    func=COPY,
+                    scale=gain32[:, t : t + 1],
+                )
+
+        def comp(g, h, s0=0, s1=PACK):
+            for s in range(s0, s1):
+                cols = slice(s * P, (s + 1) * P)
+                y_bank[(g, h, s)] = psum.tile([P, SPAN], F32, name="bank%d" % (s % 2 + 2 * Y_PAIR[4 * g + 2 * h + s // 2]))
+                nc.tensor.matmul_mx(
+                    out=y_bank[(g, h, s)][:],
+                    lhsT=codes[("lag", g)][:, cols].bitcast(FP8X4),
+                    lhsT_scale=scales[("lag", g)][:, cols],
+                    rhs=codes[("load", h)][:].bitcast(FP8X4),
+                    rhs_scale=scales[("load", h)][:],
+                    start=True,
+                    stop=True,
+                )
+
+        def y_out(g, h, s0, s1):
+            key = ("y", g, h)
+            if key not in raw:
+                raw[key] = stream.tile([P, PACK, SPAN], F32, name="y", bufs=Y_BUFS, align_bytes=64)
+            for s in range(s0, s1):
+                nc.vector.scalar_tensor_tensor(
+                    out=raw[key][:, s, :],
+                    in0=y_bank[(g, h, s)][:],
+                    scalar=weight32[:, g * PACK + s : g * PACK + s + 1],
+                    in1=xs[g][:, s, h * SPAN : (h + 1) * SPAN],
+                    op0=MULT,
+                    op1=MULT,
+                )
+
+        def y_store(g, h, s0=0, s1=PACK):
+            rows = out_0[g * SPAN : (g + 1) * SPAN, h * SPAN : (h + 1) * SPAN].rearrange("(p s) f -> p s f", s=PACK)
+            nc.sync.dma_start(out=rows[:, s0:s1, :], in_=raw[("y", g, h)][:, s0:s1, :])
+
+        def y_quantize(g, h):
+            if h == 0:
+                y_codes[g] = keep.tile([P, F], U32, name="y_codes%d" % g, align_bytes=64)
+                y_scales[g] = keep.tile([P, F], U8, name="y_scales%d" % g, align_bytes=64)
+            k = 4 * (g + 1)
+            cols = slice(h * SPAN, (h + 1) * SPAN)
+            nc.vector.quantize_mx(
+                out=y_codes[g][:, cols].bitcast(FP8X4),
+                scales=y_scales[g][k:P, cols],
+                in_=grouped[("y", g, h)][:].rearrange("p w j -> p (w j)"),
+            )
+
+        def words_store(g, lo, hi):
+            nc.sync.dma_start(
+                out=out_1[g].rearrange("p m t -> p (m t)")[:, lo * PACK : hi * PACK].bitcast(I32),
+                in_=y_codes[g][:, lo:hi].bitcast(I32),
+            )
+
+        def scales_store(g):
+            k = 4 * (g + 1)
+            for r in range(4):
+                nc.sync.dma_start(
+                    out=out_2[g, r:16:4, :].bitcast(I32), in_=y_scales[g][k + r : P : 32, :].bitcast(I32)
+                )
+
+        gain16 = keep.tile([P, PACK], BF16, name="gain16")
+        weight16 = keep.tile([P, GROUPS, PACK], BF16, name="weight16")
+        gain32 = keep.tile([P, PACK], F32, name="gain32")
+        weight32 = keep.tile([P, GROUPS * PACK], F32, name="weight32")
+        near_plane = keep.tile([P, GROUPS, R], U8, name="near_plane", align_bytes=64)
+        nc.scalar.dma_start(out=gain16[:], in_=gain.rearrange("(p t) -> p t", t=PACK))
+        nc.scalar.dma_start(out=weight16[:], in_=region_weight.rearrange("(g p s) -> p g s", p=P, s=PACK))
+        nc.vector.memset(near_plane[:].rearrange("p c n -> p (c n)").bitcast(I32), 0)
+        nc.scalar.activation(out=gain32[:], in_=gain16[:], func=COPY)
+        nc.scalar.activation(out=weight32[:], in_=weight16[:].rearrange("p g s -> p (g s)"), func=COPY)
+        load_far(0, 0)
+        load_z("zp", 0)
+        weave(("far", 0, 0), "S", 128, 512)
+        load_z("zn", 0)
+        load_far(1, 0)
+        weave(("far", 0, 0), "V", 0, 128)
+        load_z("zp", 1)
+        weave_z(("zp", 0), "S", 3, 4)
+        load_z("zn", 1)
+        weave_z(("zn", 0), "S", 3, 4)
+        weave_z(("zp", 0), "V", 0, 3)
+        load_far(2, 0)
+        weave_z(("zn", 0), "V", 0, 3)
+        load_z("zp", 2)
+        load_near_scales()
+        weave(("far", 1, 0), "V", 0, 320)
+        quantize(("zp", 0))
+        load_near(0, 1)
+        quantize(("far", 0, 0))
+        load_z("zn", 2)
+        weave(("far", 1, 0), "S", 320, 512)
+        load_far(0, 1)
+        weave_z(("zp", 1), "S", 0, 4)
+        load_far(1, 1)
+        quantize(("zn", 0))
+        load_near(1, 2)
+        weave_z(("zn", 1), "V", 0, 4)
+        quantize(("zp", 1))
+        weave(("far", 2, 0), "S", 0, 512)
+        lag_pass(0, "zp", 0, True, False)
+        quantize(("far", 1, 0))
+        load_far(2, 1)
+        weave_z(("zp", 2), "S", 3, 4)
+        weave_z(("zn", 2), "S", 3, 4)
+        lag_pass(0, "zp", 1, False, False)
+        quantize(("zn", 1))
+        weave_z(("zp", 2), "V", 0, 3)
+        lag_pass(0, "zn", 0, False, False)
+        load_far(0, 2)
+        quantize(("zp", 2))
+        load_load()
+        quantize(("far", 2, 0))
+        weave_z(("zn", 2), "V", 0, 3)
+        lag_pass(0, "zn", 1, False, False)
+        quantize(("zn", 2))
+        weave(("far", 0, 1), "V", 0, 256)
+        lag_pass(0, "zp", 2, False, False)
+        weave(("far", 1, 1), "V", 0, 384)
+        weave(("far", 0, 1), "S", 256, 512)
+        load_far(1, 2)
+        lag_pass(0, "zn", 2, False, True)
+        load_x(0)
+        load_near(2, 3)
+        weave(("far", 1, 1), "S", 384, 512)
+        lag_out(0, 0, 2)
+        quantize(("far", 0, 1))
+        lag_pass(1, "zn", 0, True, False)
+        lag_pass(1, "zp", 0, False, False)
+        lag_out(0, 2, 4)
+        weave(("far", 2, 1), "S", 448, 512)
+        quantize(("far", 1, 1))
+        weave(("lag", 0), "S", 320, 512)
+        weave(("far", 0, 2), "S", 192, 512)
+        weave(("far", 2, 1), "V", 0, 448)
+        weave(("lag", 0), "V", 0, 320)
+        weave(("far", 0, 2), "V", 0, 192)
+        load_far(2, 2)
+        lag_pass(1, "zp", 1, False, False)
+        quantize(("far", 2, 1))
+        lag_pass(1, "zn", 1, False, False)
+        lag_pass(1, "zn", 2, False, False)
+        lag_pass(1, "zp", 2, False, True)
+        quantize(("lag", 0))
+        weave(("load", 1), "S", 0, 512)
+        weave(("load", 0), "V", 0, 512)
+        quantize(("far", 0, 2))
+        load_x(1)
+        quantize(("load", 0))
+        lag_out(1, 0, 2)
+        comp(0, 0, 0, 2)
+        comp(0, 0, 2, 4)
+        weave(("far", 1, 2), "V", 0, 448)
+        quantize(("load", 1))
+        lag_out(1, 2, 4)
+        weave(("far", 1, 2), "S", 448, 512)
+        lag_pass(2, "zp", 0, True, False)
+        y_out(0, 0, 0, 2)
+        y_out(0, 0, 2, 4)
+        weave(("lag", 1), "S", 0, 512)
+        lag_pass(2, "zn", 0, False, False)
+        quantize(("far", 1, 2))
+        weave(("y", 0, 0), "V", 0, 320)
+        comp(0, 1, 0, 2)
+        y_out(0, 1, 0, 2)
+        comp(0, 1, 2, 4)
+        weave(("far", 2, 2), "S", 0, 512)
+        weave(("y", 0, 0), "S", 320, 512)
+        lag_pass(2, "zn", 1, False, False)
+        lag_pass(2, "zn", 2, False, False)
+        y_out(0, 1, 2, 4)
+        y_store(0, 0, 0, 2)
+        weave(("y", 0, 1), "S", 320, 512)
+        lag_pass(2, "zp", 1, False, False)
+        load_x(2)
+        quantize(("far", 2, 2))
+        lag_pass(2, "zp", 2, False, True)
+        quantize(("lag", 1))
+        lag_out(2, 0, 2)
+        y_store(0, 0, 2, 4)
+        weave(("y", 0, 1), "V", 0, 320)
+        y_store(0, 1, 0, 2)
+        y_store(0, 1, 2, 4)
+        comp(1, 0, 0, 2)
+        y_quantize(0, 0)
+        y_quantize(0, 1)
+        y_out(1, 0, 0, 2)
+        comp(1, 0, 2, 4)
+        lag_out(2, 2, 4)
+        weave(("lag", 2), "S", 64, 512)
+        y_out(1, 0, 2, 4)
+        comp(1, 1, 0, 2)
+        weave(("y", 1, 0), "S", 0, 512)
+        words_store(0, 0, 512)
+        weave(("lag", 2), "V", 0, 64)
+        words_store(0, 512, 1024)
+        y_store(1, 0, 0, 2)
+        y_store(1, 0, 2, 4)
+        y_out(1, 1, 0, 2)
+        comp(1, 1, 2, 4)
+        quantize(("lag", 2))
+        y_out(1, 1, 2, 4)
+        weave(("y", 1, 1), "S", 0, 512)
+        comp(2, 0, 0, 2)
+        y_out(2, 0, 0, 2)
+        comp(2, 0, 2, 4)
+        y_store(1, 1, 0, 2)
+        y_out(2, 0, 2, 4)
+        scales_store(0)
+        y_store(1, 1, 2, 4)
+        y_store(2, 0, 0, 2)
+        comp(2, 1, 0, 2)
+        y_store(2, 0, 2, 4)
+        y_out(2, 1, 0, 2)
+        y_quantize(1, 0)
+        y_store(2, 1, 0, 2)
+        comp(2, 1, 2, 4)
+        y_quantize(1, 1)
+        weave(("y", 2, 0), "S", 64, 512)
+        words_store(1, 0, 512)
+        y_out(2, 1, 2, 4)
+        weave(("y", 2, 0), "V", 0, 64)
+        weave(("y", 2, 1), "V", 0, 320)
+        scales_store(1)
+        words_store(1, 512, 1024)
+        y_quantize(2, 0)
+        y_store(2, 1, 2, 4)
+        words_store(2, 0, 512)
+        weave(("y", 2, 1), "S", 320, 512)
+        y_quantize(2, 1)
+        words_store(2, 512, 1024)
+        scales_store(2)

@@ -8,12 +8,11 @@ PACK = 4
 SPAN = P * PACK
 GROUPS = R // SPAN
 HALVES = F // SPAN
-RAW_BUFS = 10
 GROUPED_BUFS = 6
-Y_BUFS = 6
 CODE_BUFS = {"zp": 3, "zn": 3, "far": 9, "load": 2, "lag": 3}
-LAG_SET = (0, 1, 1)
-Y_PAIR = (0, 1, 0, 1, 1, 2, 0, 3, 1, 3, 0, 0)
+LAG_PAIR = (0, 1, 2, 3, 0, 2)
+Y_PAIR = (2, 1, 3, 1, 3, 1, 3, 1, 3, 1, 0, 3)
+Y_MAJOR = "ssh"
 FLOPS = 2 * (2 * R * R * C + R * C * F)
 
 F32 = mybir.dt.float32
@@ -24,6 +23,7 @@ U8 = mybir.dt.uint8
 FP8X4 = mybir.dt.float8_e4m3fn_x4
 FP4X4 = mybir.dt.float4_e2m1fn_x4
 MULT = mybir.AluOpType.mult
+ADD = mybir.AluOpType.add
 COPY = mybir.ActivationFunctionType.Copy
 
 
@@ -37,37 +37,37 @@ def tile_local_bivariate_moran_k6_kernel(
         psum = ctx.enter_context(tc.psum_pool(name="psum", bufs=1))
         ctx.enter_context(tc.manual_schedule())
 
-        raw, grouped, codes, scales = {}, {}, {}, {}
+        raw, grouped, codes, scales, z_pair, passes = {}, {}, {}, {}, {}, {}
         near, xs, lag_bank, y_bank, ys, y_codes, y_scales = {}, {}, {}, {}, {}, {}, {}
 
         def copier(engine):
             return nc.vector.tensor_copy if engine == "V" else nc.scalar.copy
 
-        def load_rows(key, rows):
-            raw[key] = stream.tile([P, PACK, SPAN], BF16, name="raw", bufs=RAW_BUFS, align_bytes=64)
-            nc.sync.dma_start(out=raw[key][:], in_=rows.rearrange("(p j) w -> p j w", j=PACK))
-
         def load_z(which, c):
+            if c not in z_pair:
+                z_pair[c] = stream.tile([P, 2, PACK, SPAN], BF16, name="zx", bufs=GROUPS, align_bytes=64)
             src = z_prev if which == "zp" else z_now
-            load_rows((which, c), src[c * SPAN : (c + 1) * SPAN, :])
+            raw[(which, c)] = z_pair[c][:, 0 if which == "zp" else 1, :, :]
+            nc.sync.dma_start(
+                out=raw[(which, c)], in_=src[c * SPAN : (c + 1) * SPAN, :].rearrange("(p j) w -> p j w", j=PACK)
+            )
 
-        def load_far(c, g):
-            load_rows(("far", c, g), far[c * SPAN : (c + 1) * SPAN, g * SPAN : (g + 1) * SPAN])
+        def load_far(c, g0, g1):
+            wide = keep.tile([P, PACK, (g1 - g0) * SPAN], BF16, name="far%d_%d" % (c, g0), align_bytes=64)
+            rows = far[c * SPAN : (c + 1) * SPAN, g0 * SPAN : g1 * SPAN]
+            nc.sync.dma_start(out=wide[:], in_=rows.rearrange("(p j) w -> p j w", j=PACK))
+            for g in range(g0, g1):
+                raw[("far", c, g)] = wide[:, :, (g - g0) * SPAN : (g - g0 + 1) * SPAN]
+
+        def load_near_pass(c):
+            near[c] = keep.tile([P, 2 * R], U8, name="near%d" % c, align_bytes=64)
+            nc.sync.dma_start(out=near[c][:].bitcast(I32), in_=near_words[c].bitcast(I32))
 
         def load_load():
             whole = keep.tile([P, PACK, F], BF16, name="load_raw", align_bytes=64)
             nc.sync.dma_start(out=whole[:], in_=load.rearrange("(p j) f -> p j f", j=PACK))
             for h in range(HALVES):
                 raw[("load", h)] = whole[:, :, h * SPAN : (h + 1) * SPAN]
-
-        def load_near(g0, g1):
-            words = keep.tile([P, GROUPS, (g1 - g0) * 2 * SPAN], U8, name="near%d" % g0, align_bytes=64)
-            nc.sync.dma_start(
-                out=words[:].bitcast(I32),
-                in_=near_words.rearrange("c p n -> p c n")[:, :, g0 * 2 * SPAN : g1 * 2 * SPAN].bitcast(I32),
-            )
-            for g in range(g0, g1):
-                near[g] = words[:, :, (g - g0) * 2 * SPAN : (g - g0 + 1) * 2 * SPAN]
 
         def load_near_scales():
             for r in range(4):
@@ -77,7 +77,7 @@ def tile_local_bivariate_moran_k6_kernel(
                 )
 
         def load_x(g):
-            xs[g] = keep.tile([P, PACK, F], BF16, name="x%d" % g, align_bytes=64)
+            xs[g] = stream.tile([P, PACK, F], BF16, name="zx", bufs=GROUPS, align_bytes=64)
             nc.sync.dma_start(
                 out=xs[g][:], in_=x[g * SPAN : (g + 1) * SPAN, :].rearrange("(p j) f -> p j f", j=PACK)
             )
@@ -88,6 +88,16 @@ def tile_local_bivariate_moran_k6_kernel(
             return grouped[key]
 
         def weave(key, engine, lo, hi):
+            if engine == "G":
+                nc.gpsimd.tensor_scalar(
+                    out=grouped_tile(key)[:, lo:hi, :],
+                    in0=raw[key][:, :, lo:hi].rearrange("p j w -> p w j"),
+                    scalar1=1.0,
+                    scalar2=-0.0,
+                    op0=MULT,
+                    op1=ADD,
+                )
+                return
             dst = grouped_tile(key)[:, lo:hi, :].rearrange("p (c i) j -> p c j i", i=4)
             src = raw[key][:, :, lo:hi].rearrange("p j (c i) -> p c j i", i=4)
             copier(engine)(out=dst, in_=src)
@@ -108,15 +118,17 @@ def tile_local_bivariate_moran_k6_kernel(
                 in_=grouped[key][:].rearrange("p w j -> p (w j)"),
             )
 
-        def lag_pass(g, which, c, first, last):
-            for t in range(PACK):
+        def lag_pass(g, b, which, c):
+            passes[(g, b)] = passes.get((g, b), 0) + 1
+            first, last = passes[(g, b)] == 1, passes[(g, b)] == 2 * GROUPS
+            for t in (2 * b, 2 * b + 1):
                 if first:
-                    lag_bank[(g, t)] = psum.tile([P, SPAN], F32, name="bank%d" % (PACK * LAG_SET[g] + t))
+                    lag_bank[(g, t)] = psum.tile([P, SPAN], F32, name="bank%d" % (2 * LAG_PAIR[2 * g + b] + t % 2))
                 cols = slice(t * P, (t + 1) * P)
                 if which == "zp":
                     rhs, rhs_scale = codes[("far", c, g)][:].bitcast(FP8X4), scales[("far", c, g)][:]
                 else:
-                    rhs, rhs_scale = near[g][:, c, :].bitcast(FP4X4), near_plane[:, c, g * SPAN : (g + 1) * SPAN]
+                    rhs, rhs_scale = near[c][:, g * 2 * SPAN : (g + 1) * 2 * SPAN].bitcast(FP4X4), near_plane[:, c, g * SPAN : (g + 1) * SPAN]
                 nc.tensor.matmul_mx(
                     out=lag_bank[(g, t)][:],
                     lhsT=codes[(which, c)][:, cols].bitcast(FP8X4),
@@ -127,10 +139,10 @@ def tile_local_bivariate_moran_k6_kernel(
                     stop=last,
                 )
 
-        def lag_out(g, t0=0, t1=PACK):
-            if t0 == 0:
+        def lag_out(g, b):
+            if ("lag", g) not in raw:
                 raw[("lag", g)] = stream.tile([P, PACK, SPAN], BF16, name="lag_raw", bufs=2, align_bytes=64)
-            for t in range(t0, t1):
+            for t in (2 * b, 2 * b + 1):
                 nc.scalar.activation(
                     out=raw[("lag", g)][:, t, :].rearrange("p (s m) -> p s m", s=PACK),
                     in_=lag_bank[(g, t)][:].rearrange("p (m s) -> p s m", s=PACK),
@@ -138,10 +150,15 @@ def tile_local_bivariate_moran_k6_kernel(
                     scale=gain32[:, t : t + 1],
                 )
 
-        def comp(g, h, s0=0, s1=PACK):
-            for s in range(s0, s1):
+        def pieces(g, u):
+            if Y_MAJOR[g] == "s":
+                return [(u, 0), (u, 1)]
+            return [(2 * (u % 2), u // 2), (2 * (u % 2) + 1, u // 2)]
+
+        def comp(g, u):
+            for n, (s, h) in enumerate(pieces(g, u)):
                 cols = slice(s * P, (s + 1) * P)
-                y_bank[(g, h, s)] = psum.tile([P, SPAN], F32, name="bank%d" % (s % 2 + 2 * Y_PAIR[4 * g + 2 * h + s // 2]))
+                y_bank[(g, h, s)] = psum.tile([P, SPAN], F32, name="bank%d" % (2 * Y_PAIR[PACK * g + u] + n))
                 nc.tensor.matmul_mx(
                     out=y_bank[(g, h, s)][:],
                     lhsT=codes[("lag", g)][:, cols].bitcast(FP8X4),
@@ -152,13 +169,18 @@ def tile_local_bivariate_moran_k6_kernel(
                     stop=True,
                 )
 
-        def y_out(g, h, s0, s1):
-            key = ("y", g, h)
-            if key not in raw:
-                raw[key] = stream.tile([P, PACK, SPAN], F32, name="y", bufs=Y_BUFS, align_bytes=64)
-            for s in range(s0, s1):
+        def y_out(g, u):
+            if u == 0:
+                if Y_MAJOR[g] == "s":
+                    ys[g] = keep.tile([P, PACK, F], F32, name="y%d" % g, align_bytes=64)
+                    for h in range(HALVES):
+                        raw[("y", g, h)] = ys[g][:, :, h * SPAN : (h + 1) * SPAN]
+                else:
+                    for h in range(HALVES):
+                        raw[("y", g, h)] = keep.tile([P, PACK, SPAN], F32, name="y%d_%d" % (g, h), align_bytes=64)
+            for s, h in pieces(g, u):
                 nc.vector.scalar_tensor_tensor(
-                    out=raw[key][:, s, :],
+                    out=raw[("y", g, h)][:, s, :],
                     in0=y_bank[(g, h, s)][:],
                     scalar=weight32[:, g * PACK + s : g * PACK + s + 1],
                     in1=xs[g][:, s, h * SPAN : (h + 1) * SPAN],
@@ -166,9 +188,13 @@ def tile_local_bivariate_moran_k6_kernel(
                     op1=MULT,
                 )
 
-        def y_store(g, h, s0=0, s1=PACK):
-            rows = out_0[g * SPAN : (g + 1) * SPAN, h * SPAN : (h + 1) * SPAN].rearrange("(p s) f -> p s f", s=PACK)
-            nc.sync.dma_start(out=rows[:, s0:s1, :], in_=raw[("y", g, h)][:, s0:s1, :])
+        def y_store(g, u0, u1):
+            rows = out_0[g * SPAN : (g + 1) * SPAN, :].rearrange("(p s) f -> p s f", s=PACK)
+            if Y_MAJOR[g] == "s":
+                nc.sync.dma_start(out=rows[:, u0:u1, :], in_=ys[g][:, u0:u1, :])
+            else:
+                h, s0, s1 = u0 // 2, 2 * (u0 % 2), 2 * ((u1 - 1) % 2) + 2
+                nc.sync.dma_start(out=rows[:, s0:s1, h * SPAN : (h + 1) * SPAN], in_=raw[("y", g, h)][:, s0:s1, :])
 
         def y_quantize(g, h):
             if h == 0:
@@ -205,164 +231,165 @@ def tile_local_bivariate_moran_k6_kernel(
         nc.vector.memset(near_plane[:].rearrange("p c n -> p (c n)").bitcast(I32), 0)
         nc.scalar.activation(out=gain32[:], in_=gain16[:], func=COPY)
         nc.scalar.activation(out=weight32[:], in_=weight16[:].rearrange("p g s -> p (g s)"), func=COPY)
-        load_far(0, 0)
+        load_far(0, 0, 2)
+        weave(("far", 0, 0), "V", 0, 64)
         load_z("zp", 0)
-        weave(("far", 0, 0), "S", 128, 512)
-        load_z("zn", 0)
-        load_far(1, 0)
-        weave(("far", 0, 0), "V", 0, 128)
+        weave(("far", 0, 1), "V", 0, 256)
         load_z("zp", 1)
-        weave_z(("zp", 0), "S", 3, 4)
-        load_z("zn", 1)
-        weave_z(("zn", 0), "S", 3, 4)
-        weave_z(("zp", 0), "V", 0, 3)
-        load_far(2, 0)
-        weave_z(("zn", 0), "V", 0, 3)
+        weave(("far", 0, 1), "S", 256, 512)
+        load_far(1, 0, 2)
+        weave(("far", 0, 0), "S", 64, 512)
+        load_z("zn", 0)
+        quantize(("far", 0, 1))
+        load_near_pass(0)
+        load_far(2, 0, 2)
         load_z("zp", 2)
         load_near_scales()
-        weave(("far", 1, 0), "V", 0, 320)
-        quantize(("zp", 0))
-        load_near(0, 1)
-        quantize(("far", 0, 0))
+        load_z("zn", 1)
         load_z("zn", 2)
-        weave(("far", 1, 0), "S", 320, 512)
-        load_far(0, 1)
-        weave_z(("zp", 1), "S", 0, 4)
-        load_far(1, 1)
-        quantize(("zn", 0))
-        load_near(1, 2)
-        weave_z(("zn", 1), "V", 0, 4)
+        weave_z(("zp", 0), "S", 3, 4)
+        weave_z(("zp", 0), "V", 0, 3)
+        weave_z(("zp", 1), "V", 0, 4)
+        load_near_pass(1)
+        load_load()
+        quantize(("far", 0, 0))
+        weave(("far", 1, 0), "V", 0, 192)
+        quantize(("zp", 0))
+        lag_pass(1, 0, "zp", 0)
+        load_near_pass(2)
+        load_far(0, 2, 3)
+        weave(("far", 1, 0), "S", 192, 512)
+        load_far(1, 2, 3)
+        lag_pass(1, 1, "zp", 0)
+        lag_pass(0, 0, "zp", 0)
+        weave(("far", 1, 1), "S", 0, 512)
         quantize(("zp", 1))
         weave(("far", 2, 0), "S", 0, 512)
-        lag_pass(0, "zp", 0, True, False)
         quantize(("far", 1, 0))
-        load_far(2, 1)
-        weave_z(("zp", 2), "S", 3, 4)
-        weave_z(("zn", 2), "S", 3, 4)
-        lag_pass(0, "zp", 1, False, False)
-        quantize(("zn", 1))
-        weave_z(("zp", 2), "V", 0, 3)
-        lag_pass(0, "zn", 0, False, False)
-        load_far(0, 2)
-        quantize(("zp", 2))
-        load_load()
-        quantize(("far", 2, 0))
-        weave_z(("zn", 2), "V", 0, 3)
-        lag_pass(0, "zn", 1, False, False)
-        quantize(("zn", 2))
-        weave(("far", 0, 1), "V", 0, 256)
-        lag_pass(0, "zp", 2, False, False)
-        weave(("far", 1, 1), "V", 0, 384)
-        weave(("far", 0, 1), "S", 256, 512)
-        load_far(1, 2)
-        lag_pass(0, "zn", 2, False, True)
-        load_x(0)
-        load_near(2, 3)
-        weave(("far", 1, 1), "S", 384, 512)
-        lag_out(0, 0, 2)
-        quantize(("far", 0, 1))
-        lag_pass(1, "zn", 0, True, False)
-        lag_pass(1, "zp", 0, False, False)
-        lag_out(0, 2, 4)
-        weave(("far", 2, 1), "S", 448, 512)
+        weave_z(("zn", 0), "V", 0, 4)
+        lag_pass(0, 1, "zp", 0)
+        quantize(("zn", 0))
+        lag_pass(0, 0, "zp", 1)
         quantize(("far", 1, 1))
-        weave(("lag", 0), "S", 320, 512)
-        weave(("far", 0, 2), "S", 192, 512)
-        weave(("far", 2, 1), "V", 0, 448)
-        weave(("lag", 0), "V", 0, 320)
-        weave(("far", 0, 2), "V", 0, 192)
-        load_far(2, 2)
-        lag_pass(1, "zp", 1, False, False)
+        lag_pass(1, 0, "zp", 1)
+        weave(("far", 2, 1), "V", 0, 512)
+        weave_z(("zn", 1), "S", 0, 4)
+        weave_z(("zp", 2), "V", 0, 4)
+        lag_pass(0, 1, "zp", 1)
+        lag_pass(1, 0, "zn", 0)
+        lag_pass(1, 1, "zp", 1)
+        weave(("load", 1), "S", 192, 512)
+        quantize(("far", 2, 0))
+        quantize(("zp", 2))
+        lag_pass(0, 0, "zn", 0)
+        lag_pass(0, 1, "zp", 2)
         quantize(("far", 2, 1))
-        lag_pass(1, "zn", 1, False, False)
-        lag_pass(1, "zn", 2, False, False)
-        lag_pass(1, "zp", 2, False, True)
-        quantize(("lag", 0))
-        weave(("load", 1), "S", 0, 512)
+        weave_z(("zn", 2), "V", 0, 4)
+        lag_pass(0, 0, "zp", 2)
+        lag_pass(0, 1, "zn", 0)
+        lag_pass(1, 1, "zn", 0)
+        quantize(("zn", 1))
+        lag_pass(1, 0, "zp", 2)
+        quantize(("zn", 2))
+        lag_pass(0, 0, "zn", 1)
+        lag_pass(1, 0, "zn", 1)
         weave(("load", 0), "V", 0, 512)
-        quantize(("far", 0, 2))
-        load_x(1)
+        weave(("load", 1), "V", 0, 192)
         quantize(("load", 0))
-        lag_out(1, 0, 2)
-        comp(0, 0, 0, 2)
-        comp(0, 0, 2, 4)
-        weave(("far", 1, 2), "V", 0, 448)
         quantize(("load", 1))
-        lag_out(1, 2, 4)
-        weave(("far", 1, 2), "S", 448, 512)
-        lag_pass(2, "zp", 0, True, False)
-        y_out(0, 0, 0, 2)
-        y_out(0, 0, 2, 4)
-        weave(("lag", 1), "S", 0, 512)
-        lag_pass(2, "zn", 0, False, False)
+        lag_pass(0, 0, "zn", 2)
+        weave(("far", 0, 2), "V", 0, 512)
+        load_x(0)
+        lag_pass(0, 1, "zn", 1)
+        lag_pass(0, 1, "zn", 2)
+        lag_out(0, 0)
+        lag_out(0, 1)
+        weave(("lag", 0), "S", 320, 512)
+        lag_pass(1, 0, "zn", 2)
+        lag_pass(2, 0, "zn", 0)
+        lag_pass(1, 1, "zn", 1)
+        lag_pass(1, 1, "zn", 2)
+        lag_pass(1, 1, "zp", 2)
+        weave(("lag", 0), "V", 0, 320)
+        lag_out(1, 0)
+        lag_out(1, 1)
+        quantize(("far", 0, 2))
+        quantize(("lag", 0))
+        load_far(2, 2, 3)
+        lag_pass(2, 0, "zn", 1)
+        weave(("far", 1, 2), "V", 0, 320)
+        comp(0, 0)
+        y_out(0, 0)
+        lag_pass(2, 0, "zp", 0)
+        comp(0, 1)
+        y_out(0, 1)
+        comp(0, 2)
+        y_out(0, 2)
+        weave(("far", 1, 2), "S", 320, 512)
+        lag_pass(2, 1, "zp", 0)
+        lag_pass(2, 1, "zn", 0)
+        comp(0, 3)
+        lag_pass(2, 1, "zn", 1)
         quantize(("far", 1, 2))
-        weave(("y", 0, 0), "V", 0, 320)
-        comp(0, 1, 0, 2)
-        y_out(0, 1, 0, 2)
-        comp(0, 1, 2, 4)
-        weave(("far", 2, 2), "S", 0, 512)
-        weave(("y", 0, 0), "S", 320, 512)
-        lag_pass(2, "zn", 1, False, False)
-        lag_pass(2, "zn", 2, False, False)
-        y_out(0, 1, 2, 4)
-        y_store(0, 0, 0, 2)
-        weave(("y", 0, 1), "S", 320, 512)
-        lag_pass(2, "zp", 1, False, False)
-        load_x(2)
-        quantize(("far", 2, 2))
-        lag_pass(2, "zp", 2, False, True)
+        load_x(1)
+        lag_pass(2, 0, "zn", 2)
+        weave(("lag", 1), "S", 0, 512)
         quantize(("lag", 1))
-        lag_out(2, 0, 2)
-        y_store(0, 0, 2, 4)
-        weave(("y", 0, 1), "V", 0, 320)
-        y_store(0, 1, 0, 2)
-        y_store(0, 1, 2, 4)
-        comp(1, 0, 0, 2)
-        y_quantize(0, 0)
-        y_quantize(0, 1)
-        y_out(1, 0, 0, 2)
-        comp(1, 0, 2, 4)
-        lag_out(2, 2, 4)
-        weave(("lag", 2), "S", 64, 512)
-        y_out(1, 0, 2, 4)
-        comp(1, 1, 0, 2)
-        weave(("y", 1, 0), "S", 0, 512)
-        words_store(0, 0, 512)
-        weave(("lag", 2), "V", 0, 64)
-        words_store(0, 512, 1024)
-        y_store(1, 0, 0, 2)
-        y_store(1, 0, 2, 4)
-        y_out(1, 1, 0, 2)
-        comp(1, 1, 2, 4)
-        quantize(("lag", 2))
-        y_out(1, 1, 2, 4)
+        y_out(0, 3)
+        lag_pass(2, 0, "zp", 1)
+        comp(1, 0)
+        y_out(1, 0)
+        lag_pass(2, 1, "zn", 2)
+        weave(("far", 2, 2), "S", 0, 512)
+        quantize(("far", 2, 2))
+        comp(1, 1)
+        comp(1, 2)
+        weave(("y", 0, 0), "S", 64, 512)
+        y_out(1, 1)
+        lag_pass(2, 0, "zp", 2)
+        weave(("y", 0, 0), "V", 0, 64)
+        lag_pass(2, 1, "zp", 1)
+        lag_pass(2, 1, "zp", 2)
+        lag_out(2, 0)
+        comp(1, 3)
+        y_out(1, 2)
+        y_out(1, 3)
+        load_x(2)
+        lag_out(2, 1)
+        weave(("lag", 2), "V", 0, 512)
+        y_store(0, 0, 2)
+        y_store(0, 2, 4)
+        y_store(1, 0, 2)
+        y_store(1, 2, 4)
+        weave(("y", 0, 1), "S", 0, 512)
+        weave(("y", 1, 0), "S", 128, 512)
         weave(("y", 1, 1), "S", 0, 512)
-        comp(2, 0, 0, 2)
-        y_out(2, 0, 0, 2)
-        comp(2, 0, 2, 4)
-        y_store(1, 1, 0, 2)
-        y_out(2, 0, 2, 4)
+        y_quantize(0, 0)
+        quantize(("lag", 2))
+        comp(2, 0)
+        comp(2, 1)
+        comp(2, 2)
+        y_quantize(0, 1)
+        words_store(0, 0, 1024)
         scales_store(0)
-        y_store(1, 1, 2, 4)
-        y_store(2, 0, 0, 2)
-        comp(2, 1, 0, 2)
-        y_store(2, 0, 2, 4)
-        y_out(2, 1, 0, 2)
+        weave(("y", 1, 0), "V", 0, 128)
+        y_out(2, 0)
+        comp(2, 3)
+        y_out(2, 1)
+        y_store(2, 0, 1)
+        y_store(2, 1, 2)
+        y_out(2, 2)
+        y_store(2, 2, 3)
         y_quantize(1, 0)
-        y_store(2, 1, 0, 2)
-        comp(2, 1, 2, 4)
         y_quantize(1, 1)
-        weave(("y", 2, 0), "S", 64, 512)
-        words_store(1, 0, 512)
-        y_out(2, 1, 2, 4)
-        weave(("y", 2, 0), "V", 0, 64)
-        weave(("y", 2, 1), "V", 0, 320)
+        weave(("y", 2, 0), "S", 0, 512)
         scales_store(1)
-        words_store(1, 512, 1024)
+        words_store(1, 0, 1024)
+        y_out(2, 3)
+        weave(("y", 2, 1), "V", 0, 512)
         y_quantize(2, 0)
-        y_store(2, 1, 2, 4)
-        words_store(2, 0, 512)
-        weave(("y", 2, 1), "S", 320, 512)
+        y_store(2, 3, 4)
         y_quantize(2, 1)
+        words_store(2, 0, 512)
         words_store(2, 512, 1024)
         scales_store(2)

@@ -1,19 +1,18 @@
 from contextlib import ExitStack
 
 import concourse.mybir as mybir
+from concourse.masks import make_identity
 
-R, C, F = 1536, 512, 1024
+REGIONS, INDICATORS, COMPOSITES = 1536, 512, 1024
+FLOPS = 2 * (2 * REGIONS * REGIONS * INDICATORS + REGIONS * INDICATORS * COMPOSITES)
+
 P = 128
 PACK = 4
 SPAN = P * PACK
-GROUPS = R // SPAN
-HALVES = F // SPAN
-GROUPED_BUFS = 6
-CODE_BUFS = {"zp": 3, "zn": 3, "far": 9, "load": 2, "lag": 3}
-LAG_PAIR = (0, 1, 2, 3, 0, 2)
-Y_PAIR = (2, 1, 3, 1, 3, 1, 3, 1, 3, 1, 0, 3)
-Y_MAJOR = "ssh"
-FLOPS = 2 * (2 * R * R * C + R * C * F)
+SPANS = REGIONS // SPAN
+HALVES = COMPOSITES // SPAN
+EIGHTH = SPAN // 8
+LAST = SPANS - 1
 
 F32 = mybir.dt.float32
 BF16 = mybir.dt.bfloat16
@@ -26,48 +25,56 @@ MULT = mybir.AluOpType.mult
 ADD = mybir.AluOpType.add
 COPY = mybir.ActivationFunctionType.Copy
 
+STAGING = (
+    (("z_prev", 0), ("far", 1, 1), ("load", 1), ("y", 0, 1), ("y", 1, 1)),
+    (("far", 0, 0), ("z_now", 1), ("load", 0), ("lag", 2)),
+    (("far", 0, 1), ("far", 2, 0), ("far", 0, 2), ("far", 1, 2), ("y", 2, 1)),
+    (("z_now", 0), ("far", 2, 1), ("lag", 0), ("y", 1, 0)),
+    (("z_prev", 1), ("z_prev", 2), ("lag", 1), ("y", 2, 0)),
+    (("far", 1, 0), ("z_now", 2), ("far", 2, 2), ("y", 0, 0)),
+)
+
+LAG_PAIRS = ((0, 1), (2, 3), (0, 1))
+Y_PAIRS = ((2, 3, 2, 3), (2, 3, 2, 3), (0, 1, 2, 3))
+
 
 def tile_local_bivariate_moran_k6_kernel(
     tc, far, z_prev, near_words, near_scales, z_now, gain, load, x, region_weight, out_0, out_1, out_2
 ):
     nc = tc.nc
     with ExitStack() as ctx:
-        keep = ctx.enter_context(tc.tile_pool(name="keep", bufs=1))
-        stream = ctx.enter_context(tc.tile_pool(name="stream", bufs=1))
+        sbuf = ctx.enter_context(tc.tile_pool(name="sbuf", bufs=1))
         psum = ctx.enter_context(tc.psum_pool(name="psum", bufs=1))
         ctx.enter_context(tc.manual_schedule())
 
-        raw, grouped, codes, scales, z_pair, passes = {}, {}, {}, {}, {}, {}
-        near, xs, lag_bank, y_bank, ys, y_codes, y_scales = {}, {}, {}, {}, {}, {}, {}
+        rows = {}
+        staged = {}
+        words, scales = {}, {}
+        z_tiles, near, x_tiles, y_tiles, y_words, y_scales = {}, {}, {}, {}, {}, {}
+        lag_banks, lag_passes, y_banks = {}, {}, {}
 
-        def copier(engine):
-            return nc.vector.tensor_copy if engine == "V" else nc.scalar.copy
+        def bank(pair, n, shape, dtype):
+            return psum.tile(shape, dtype, name="bank%d" % (2 * pair + n))
 
-        def load_z(which, c):
-            if c not in z_pair:
-                z_pair[c] = stream.tile([P, 2, PACK, SPAN], BF16, name="zx", bufs=GROUPS, align_bytes=64)
-            src = z_prev if which == "zp" else z_now
-            raw[(which, c)] = z_pair[c][:, 0 if which == "zp" else 1, :, :]
-            nc.sync.dma_start(
-                out=raw[(which, c)], in_=src[c * SPAN : (c + 1) * SPAN, :].rearrange("(p j) w -> p j w", j=PACK)
-            )
+        def by_word(hbm_rows):
+            return hbm_rows.rearrange("(p j) w -> p j w", j=PACK)
+
+        def load_z(name, c):
+            if c not in z_tiles:
+                z_tiles[c] = sbuf.tile([P, 2, PACK, INDICATORS], BF16, name="z_then_x", bufs=SPANS, align_bytes=64)
+            source, place = (z_prev, 0) if name == "z_prev" else (z_now, 1)
+            rows[(name, c)] = z_tiles[c][:, place, :, :]
+            nc.sync.dma_start(out=rows[(name, c)], in_=by_word(source[c * SPAN : (c + 1) * SPAN, :]))
 
         def load_far(c, g0, g1):
-            wide = keep.tile([P, PACK, (g1 - g0) * SPAN], BF16, name="far%d_%d" % (c, g0), align_bytes=64)
-            rows = far[c * SPAN : (c + 1) * SPAN, g0 * SPAN : g1 * SPAN]
-            nc.sync.dma_start(out=wide[:], in_=rows.rearrange("(p j) w -> p j w", j=PACK))
+            tile = sbuf.tile([P, PACK, (g1 - g0) * SPAN], BF16, name="far%d_%d" % (c, g0), align_bytes=64)
+            nc.sync.dma_start(out=tile[:], in_=by_word(far[c * SPAN : (c + 1) * SPAN, g0 * SPAN : g1 * SPAN]))
             for g in range(g0, g1):
-                raw[("far", c, g)] = wide[:, :, (g - g0) * SPAN : (g - g0 + 1) * SPAN]
+                rows[("far", c, g)] = tile[:, :, (g - g0) * SPAN : (g - g0 + 1) * SPAN]
 
-        def load_near_pass(c):
-            near[c] = keep.tile([P, 2 * R], U8, name="near%d" % c, align_bytes=64)
+        def load_near(c):
+            near[c] = sbuf.tile([P, 2 * REGIONS], U8, name="near%d" % c, align_bytes=64)
             nc.sync.dma_start(out=near[c][:].bitcast(I32), in_=near_words[c].bitcast(I32))
-
-        def load_load():
-            whole = keep.tile([P, PACK, F], BF16, name="load_raw", align_bytes=64)
-            nc.sync.dma_start(out=whole[:], in_=load.rearrange("(p j) f -> p j f", j=PACK))
-            for h in range(HALVES):
-                raw[("load", h)] = whole[:, :, h * SPAN : (h + 1) * SPAN]
 
         def load_near_scales():
             for r in range(4):
@@ -76,320 +83,326 @@ def tile_local_bivariate_moran_k6_kernel(
                     in_=near_scales[:, r:16:4, :].rearrange("c q n -> q c n").bitcast(I32),
                 )
 
+        def load_load():
+            tile = sbuf.tile([P, PACK, COMPOSITES], BF16, name="load", align_bytes=64)
+            nc.sync.dma_start(out=tile[:], in_=by_word(load))
+            for h in range(HALVES):
+                rows[("load", h)] = tile[:, :, h * SPAN : (h + 1) * SPAN]
+
         def load_x(g):
-            xs[g] = stream.tile([P, PACK, F], BF16, name="zx", bufs=GROUPS, align_bytes=64)
-            nc.sync.dma_start(
-                out=xs[g][:], in_=x[g * SPAN : (g + 1) * SPAN, :].rearrange("(p j) f -> p j f", j=PACK)
-            )
+            x_tiles[g] = sbuf.tile([P, PACK, COMPOSITES], BF16, name="z_then_x", bufs=SPANS, align_bytes=64)
+            nc.sync.dma_start(out=x_tiles[g][:], in_=by_word(x[g * SPAN : (g + 1) * SPAN, :]))
 
-        def grouped_tile(key):
-            if key not in grouped:
-                grouped[key] = stream.tile([P, SPAN, PACK], BF16, name="grouped", bufs=GROUPED_BUFS, align_bytes=64)
-            return grouped[key]
-
-        def weave(key, engine, lo, hi):
-            if engine == "G":
+        def interleave(key, engine, lo, hi):
+            if key not in staged:
+                buffer = [n for n, keys in enumerate(STAGING) if key in keys][0]
+                staged[key] = sbuf.tile([P, SPAN, PACK], BF16, name="staged%d" % buffer, align_bytes=64)
+            cols = slice(lo * EIGHTH, hi * EIGHTH)
+            if engine == "gpsimd":
+                src = rows[key][:, :, cols].rearrange("p j w -> p w j")
                 nc.gpsimd.tensor_scalar(
-                    out=grouped_tile(key)[:, lo:hi, :],
-                    in0=raw[key][:, :, lo:hi].rearrange("p j w -> p w j"),
-                    scalar1=1.0,
-                    scalar2=-0.0,
-                    op0=MULT,
-                    op1=ADD,
+                    out=staged[key][:, cols, :], in0=src, scalar1=1.0, scalar2=-0.0, op0=MULT, op1=ADD
                 )
                 return
-            dst = grouped_tile(key)[:, lo:hi, :].rearrange("p (c i) j -> p c j i", i=4)
-            src = raw[key][:, :, lo:hi].rearrange("p j (c i) -> p c j i", i=4)
-            copier(engine)(out=dst, in_=src)
+            if key[0] in ("z_prev", "z_now"):
+                ts = slice(lo // 2, hi // 2)
+                dst = staged[key][:].rearrange("p (t a b) j -> p a t b j", t=PACK, b=2)[:, :, ts, :, :]
+                src = rows[key].rearrange("p j (a b t) -> p a t b j", t=PACK, b=2)[:, :, ts, :, :]
+            else:
+                dst = staged[key][:, cols, :].rearrange("p (a i) j -> p a j i", i=4)
+                src = rows[key][:, :, cols].rearrange("p j (a i) -> p a j i", i=4)
+            copy = nc.vector.tensor_copy if engine == "vector" else nc.scalar.copy
+            copy(out=dst, in_=src)
 
-        def weave_z(key, engine, t0, t1):
-            dst = grouped_tile(key)[:].rearrange("p (t a b) j -> p a t b j", t=PACK, b=2)[:, :, t0:t1, :, :]
-            src = raw[key][:].rearrange("p j (a b t) -> p a t b j", t=PACK, b=2)[:, :, t0:t1, :, :]
-            copier(engine)(out=dst, in_=src)
+        def share(key, cut):
+            interleave(key, "scalar", cut, 8)
+            interleave(key, "vector", 0, cut)
 
         def quantize(key):
-            tag = key[0]
-            bufs = CODE_BUFS[tag]
-            codes[key] = stream.tile([P, SPAN], U32, name=tag + "_codes", bufs=bufs, align_bytes=64)
-            scales[key] = stream.tile([P, SPAN], U8, name=tag + "_scales", bufs=bufs, align_bytes=64)
+            name = "_".join(str(part) for part in key)
+            words[key] = sbuf.tile([P, SPAN], U32, name=name + "_words", align_bytes=64)
+            scales[key] = sbuf.tile([P, SPAN], U8, name=name + "_scales", align_bytes=64)
             nc.vector.quantize_mx(
-                out=codes[key][:].bitcast(FP8X4),
+                out=words[key][:].bitcast(FP8X4),
                 scales=scales[key][:],
-                in_=grouped[key][:].rearrange("p w j -> p (w j)"),
+                in_=staged[key][:].rearrange("p w j -> p (w j)"),
             )
 
-        def lag_pass(g, b, which, c):
-            passes[(g, b)] = passes.get((g, b), 0) + 1
-            first, last = passes[(g, b)] == 1, passes[(g, b)] == 2 * GROUPS
-            for t in (2 * b, 2 * b + 1):
+        def lag_pass(g, b, name, c):
+            lag_passes[(g, b)] = lag_passes.get((g, b), 0) + 1
+            first, last = lag_passes[(g, b)] == 1, lag_passes[(g, b)] == 2 * SPANS
+            if name == "z_prev":
+                moving = words[("far", c, g)][:].bitcast(FP8X4)
+                moving_scale = scales[("far", c, g)][:]
+            else:
+                moving = near[c][:, 2 * g * SPAN : 2 * (g + 1) * SPAN].bitcast(FP4X4)
+                moving_scale = near_plane[:, c, g * SPAN : (g + 1) * SPAN]
+            for n in range(2):
+                t = 2 * b + n
                 if first:
-                    lag_bank[(g, t)] = psum.tile([P, SPAN], F32, name="bank%d" % (2 * LAG_PAIR[2 * g + b] + t % 2))
+                    lag_banks[(g, t)] = bank(LAG_PAIRS[g][b], n, [P, SPAN], F32)
                 cols = slice(t * P, (t + 1) * P)
-                if which == "zp":
-                    rhs, rhs_scale = codes[("far", c, g)][:].bitcast(FP8X4), scales[("far", c, g)][:]
-                else:
-                    rhs, rhs_scale = near[c][:, g * 2 * SPAN : (g + 1) * 2 * SPAN].bitcast(FP4X4), near_plane[:, c, g * SPAN : (g + 1) * SPAN]
                 nc.tensor.matmul_mx(
-                    out=lag_bank[(g, t)][:],
-                    lhsT=codes[(which, c)][:, cols].bitcast(FP8X4),
-                    lhsT_scale=scales[(which, c)][:, cols],
-                    rhs=rhs,
-                    rhs_scale=rhs_scale,
+                    out=lag_banks[(g, t)][:],
+                    lhsT=words[(name, c)][:, cols].bitcast(FP8X4),
+                    lhsT_scale=scales[(name, c)][:, cols],
+                    rhs=moving,
+                    rhs_scale=moving_scale,
                     start=first,
                     stop=last,
                 )
 
-        def lag_out(g, b):
-            if ("lag", g) not in raw:
-                raw[("lag", g)] = stream.tile([P, PACK, SPAN], BF16, name="lag_raw", bufs=2, align_bytes=64)
-            for t in (2 * b, 2 * b + 1):
+        def lag_span(g, name, c):
+            for b in range(2):
+                lag_pass(g, b, name, c)
+
+        def lag_out(g):
+            rows[("lag", g)] = sbuf.tile([P, PACK, SPAN], BF16, name="lag", bufs=2, align_bytes=64)
+            for t in range(PACK):
                 nc.scalar.activation(
-                    out=raw[("lag", g)][:, t, :].rearrange("p (s m) -> p s m", s=PACK),
-                    in_=lag_bank[(g, t)][:].rearrange("p (m s) -> p s m", s=PACK),
+                    out=rows[("lag", g)][:, t, :].rearrange("p (s m) -> p s m", s=PACK),
+                    in_=lag_banks[(g, t)][:].rearrange("p (m s) -> p s m", s=PACK),
                     func=COPY,
-                    scale=gain32[:, t : t + 1],
+                    scale=factors[:, t, SPANS : SPANS + 1],
                 )
 
-        def pieces(g, u):
-            if Y_MAJOR[g] == "s":
+        def quarter(g, u):
+            if g < LAST:
                 return [(u, 0), (u, 1)]
             return [(2 * (u % 2), u // 2), (2 * (u % 2) + 1, u // 2)]
 
         def comp(g, u):
-            for n, (s, h) in enumerate(pieces(g, u)):
+            for n, (s, h) in enumerate(quarter(g, u)):
                 cols = slice(s * P, (s + 1) * P)
-                y_bank[(g, h, s)] = psum.tile([P, SPAN], F32, name="bank%d" % (2 * Y_PAIR[PACK * g + u] + n))
+                y_banks[(g, s, h)] = bank(Y_PAIRS[g][u], n, [P, SPAN], F32)
                 nc.tensor.matmul_mx(
-                    out=y_bank[(g, h, s)][:],
-                    lhsT=codes[("lag", g)][:, cols].bitcast(FP8X4),
+                    out=y_banks[(g, s, h)][:],
+                    lhsT=words[("lag", g)][:, cols].bitcast(FP8X4),
                     lhsT_scale=scales[("lag", g)][:, cols],
-                    rhs=codes[("load", h)][:].bitcast(FP8X4),
+                    rhs=words[("load", h)][:].bitcast(FP8X4),
                     rhs_scale=scales[("load", h)][:],
                     start=True,
                     stop=True,
                 )
 
         def y_out(g, u):
-            if u == 0:
-                if Y_MAJOR[g] == "s":
-                    ys[g] = keep.tile([P, PACK, F], F32, name="y%d" % g, align_bytes=64)
-                    for h in range(HALVES):
-                        raw[("y", g, h)] = ys[g][:, :, h * SPAN : (h + 1) * SPAN]
-                else:
-                    for h in range(HALVES):
-                        raw[("y", g, h)] = keep.tile([P, PACK, SPAN], F32, name="y%d_%d" % (g, h), align_bytes=64)
-            for s, h in pieces(g, u):
+            if u == 0 and g < LAST:
+                y_tiles[g] = sbuf.tile([P, PACK, COMPOSITES], F32, name="y%d" % g, align_bytes=64)
+                for h in range(HALVES):
+                    rows[("y", g, h)] = y_tiles[g][:, :, h * SPAN : (h + 1) * SPAN]
+            if u == 0 and g == LAST:
+                for h in range(HALVES):
+                    rows[("y", g, h)] = sbuf.tile([P, PACK, SPAN], F32, name="y%d_%d" % (g, h), align_bytes=64)
+            for s, h in quarter(g, u):
                 nc.vector.scalar_tensor_tensor(
-                    out=raw[("y", g, h)][:, s, :],
-                    in0=y_bank[(g, h, s)][:],
-                    scalar=weight32[:, g * PACK + s : g * PACK + s + 1],
-                    in1=xs[g][:, s, h * SPAN : (h + 1) * SPAN],
+                    out=rows[("y", g, h)][:, s, :],
+                    in0=y_banks[(g, s, h)][:],
+                    scalar=factors[:, s, g : g + 1],
+                    in1=x_tiles[g][:, s, h * SPAN : (h + 1) * SPAN],
                     op0=MULT,
                     op1=MULT,
                 )
 
-        def y_store(g, u0, u1):
-            rows = out_0[g * SPAN : (g + 1) * SPAN, :].rearrange("(p s) f -> p s f", s=PACK)
-            if Y_MAJOR[g] == "s":
-                nc.sync.dma_start(out=rows[:, u0:u1, :], in_=ys[g][:, u0:u1, :])
-            else:
-                h, s0, s1 = u0 // 2, 2 * (u0 % 2), 2 * ((u1 - 1) % 2) + 2
-                nc.sync.dma_start(out=rows[:, s0:s1, h * SPAN : (h + 1) * SPAN], in_=raw[("y", g, h)][:, s0:s1, :])
+        def plane_row(g):
+            return 4 * (g + 1)
 
         def y_quantize(g, h):
             if h == 0:
-                y_codes[g] = keep.tile([P, F], U32, name="y_codes%d" % g, align_bytes=64)
-                y_scales[g] = keep.tile([P, F], U8, name="y_scales%d" % g, align_bytes=64)
-            k = 4 * (g + 1)
+                y_words[g] = sbuf.tile([P, COMPOSITES], U32, name="y_words%d" % g, align_bytes=64)
+                y_scales[g] = sbuf.tile([P, COMPOSITES], U8, name="y_scales%d" % g, align_bytes=64)
             cols = slice(h * SPAN, (h + 1) * SPAN)
             nc.vector.quantize_mx(
-                out=y_codes[g][:, cols].bitcast(FP8X4),
-                scales=y_scales[g][k:P, cols],
-                in_=grouped[("y", g, h)][:].rearrange("p w j -> p (w j)"),
+                out=y_words[g][:, cols].bitcast(FP8X4),
+                scales=y_scales[g][plane_row(g) : P, cols],
+                in_=staged[("y", g, h)][:].rearrange("p w j -> p (w j)"),
             )
 
-        def words_store(g, lo, hi):
-            nc.sync.dma_start(
-                out=out_1[g].rearrange("p m t -> p (m t)")[:, lo * PACK : hi * PACK].bitcast(I32),
-                in_=y_codes[g][:, lo:hi].bitcast(I32),
-            )
+        def store_y_rows(g, s0, s1):
+            hbm = by_word(out_0[g * SPAN : (g + 1) * SPAN, :])
+            nc.sync.dma_start(out=hbm[:, s0:s1, :], in_=y_tiles[g][:, s0:s1, :])
 
-        def scales_store(g):
-            k = 4 * (g + 1)
+        def store_y_half_rows(g, h, s0, s1):
+            hbm = by_word(out_0[g * SPAN : (g + 1) * SPAN, :])
+            nc.sync.dma_start(out=hbm[:, s0:s1, h * SPAN : (h + 1) * SPAN], in_=rows[("y", g, h)][:, s0:s1, :])
+
+        def store_words(g, h0, h1):
+            hbm = out_1[g].rearrange("p m j -> p (m j)")[:, h0 * SPAN * PACK : h1 * SPAN * PACK]
+            nc.sync.dma_start(out=hbm.bitcast(I32), in_=y_words[g][:, h0 * SPAN : h1 * SPAN].bitcast(I32))
+
+        def store_scales(g):
             for r in range(4):
                 nc.sync.dma_start(
-                    out=out_2[g, r:16:4, :].bitcast(I32), in_=y_scales[g][k + r : P : 32, :].bitcast(I32)
+                    out=out_2[g, r:16:4, :].bitcast(I32), in_=y_scales[g][plane_row(g) + r : P : 32, :].bitcast(I32)
                 )
 
-        gain16 = keep.tile([P, PACK], BF16, name="gain16")
-        weight16 = keep.tile([P, GROUPS, PACK], BF16, name="weight16")
-        gain32 = keep.tile([P, PACK], F32, name="gain32")
-        weight32 = keep.tile([P, GROUPS * PACK], F32, name="weight32")
-        near_plane = keep.tile([P, GROUPS, R], U8, name="near_plane", align_bytes=64)
-        nc.scalar.dma_start(out=gain16[:], in_=gain.rearrange("(p t) -> p t", t=PACK))
-        nc.scalar.dma_start(out=weight16[:], in_=region_weight.rearrange("(g p s) -> p g s", p=P, s=PACK))
+        vectors = sbuf.tile([P, SPAN], BF16, name="vectors", align_bytes=64)
+        identity = sbuf.tile([P, P], BF16, name="identity", align_bytes=64)
+        factors = sbuf.tile([P, PACK, SPANS + 1], F32, name="factors")
+        near_plane = sbuf.tile([P, SPANS, REGIONS], U8, name="near_plane", align_bytes=64)
+        make_identity(nc, identity[:])
+        nc.vector.memset(vectors[:].bitcast(I32), 0)
         nc.vector.memset(near_plane[:].rearrange("p c n -> p (c n)").bitcast(I32), 0)
-        nc.scalar.activation(out=gain32[:], in_=gain16[:], func=COPY)
-        nc.scalar.activation(out=weight32[:], in_=weight16[:].rearrange("p g s -> p (g s)"), func=COPY)
+
+        def load_vectors():
+            weight_rows = region_weight.rearrange("(g n) -> g n", g=SPANS)
+            nc.sync.dma_start(out=vectors[0:LAST, :], in_=weight_rows[0:LAST, :])
+            nc.sync.dma_start(out=vectors[LAST:SPANS, :], in_=weight_rows[LAST:SPANS, :])
+            nc.sync.dma_start(out=vectors[SPANS : SPANS + 1, :], in_=gain.rearrange("(o n) -> o n", o=1))
+
+        def turn_vectors():
+            turned = bank(LAG_PAIRS[1][1], 1, [P, PACK, P], BF16)
+            for s in range(PACK):
+                nc.tensor.transpose(turned[:, s, :], vectors[:, s:SPAN:PACK], identity[:])
+            nc.scalar.activation(out=factors[:], in_=turned[:, :, 0 : SPANS + 1], func=COPY)
+
+        load_z("z_prev", 0)
+        load_vectors()
         load_far(0, 0, 2)
-        weave(("far", 0, 0), "V", 0, 64)
-        load_z("zp", 0)
-        weave(("far", 0, 1), "V", 0, 256)
-        load_z("zp", 1)
-        weave(("far", 0, 1), "S", 256, 512)
+        load_z("z_now", 0)
+        load_z("z_prev", 1)
         load_far(1, 0, 2)
-        weave(("far", 0, 0), "S", 64, 512)
-        load_z("zn", 0)
-        quantize(("far", 0, 1))
-        load_near_pass(0)
-        load_far(2, 0, 2)
-        load_z("zp", 2)
+        load_near(0)
         load_near_scales()
-        load_z("zn", 1)
-        load_z("zn", 2)
-        weave_z(("zp", 0), "S", 3, 4)
-        weave_z(("zp", 0), "V", 0, 3)
-        weave_z(("zp", 1), "V", 0, 4)
-        load_near_pass(1)
+        load_z("z_now", 1)
+        load_far(2, 0, 2)
+        load_z("z_prev", 2)
+        load_near(1)
+        load_z("z_now", 2)
         load_load()
+        load_near(2)
+
+        share(("z_prev", 0), 4)
+        turn_vectors()
+        quantize(("z_prev", 0))
+        share(("far", 0, 0), 4)
+        share(("far", 0, 1), 4)
         quantize(("far", 0, 0))
-        weave(("far", 1, 0), "V", 0, 192)
-        quantize(("zp", 0))
-        lag_pass(1, 0, "zp", 0)
-        load_near_pass(2)
-        load_far(0, 2, 3)
-        weave(("far", 1, 0), "S", 192, 512)
-        load_far(1, 2, 3)
-        lag_pass(1, 1, "zp", 0)
-        lag_pass(0, 0, "zp", 0)
-        weave(("far", 1, 1), "S", 0, 512)
-        quantize(("zp", 1))
-        weave(("far", 2, 0), "S", 0, 512)
+        share(("z_now", 0), 4)
+        quantize(("far", 0, 1))
+        lag_span(0, "z_prev", 0)
+        lag_span(1, "z_prev", 0)
+        share(("z_prev", 1), 4)
+        quantize(("z_now", 0))
+        share(("far", 1, 0), 4)
+        quantize(("z_prev", 1))
+        share(("far", 1, 1), 4)
         quantize(("far", 1, 0))
-        weave_z(("zn", 0), "V", 0, 4)
-        lag_pass(0, 1, "zp", 0)
-        quantize(("zn", 0))
-        lag_pass(0, 0, "zp", 1)
+        lag_span(0, "z_prev", 1)
+        lag_span(0, "z_now", 0)
+        lag_span(1, "z_now", 0)
+        share(("z_now", 1), 4)
         quantize(("far", 1, 1))
-        lag_pass(1, 0, "zp", 1)
-        weave(("far", 2, 1), "V", 0, 512)
-        weave_z(("zn", 1), "S", 0, 4)
-        weave_z(("zp", 2), "V", 0, 4)
-        lag_pass(0, 1, "zp", 1)
-        lag_pass(1, 0, "zn", 0)
-        lag_pass(1, 1, "zp", 1)
-        weave(("load", 1), "S", 192, 512)
+        lag_span(1, "z_prev", 1)
+        quantize(("z_now", 1))
+
+        share(("far", 2, 0), 2)
+        interleave(("far", 2, 1), "vector", 0, 6)
+        share(("z_prev", 2), 6)
+        interleave(("far", 2, 1), "scalar", 6, 8)
         quantize(("far", 2, 0))
-        quantize(("zp", 2))
-        lag_pass(0, 0, "zn", 0)
-        lag_pass(0, 1, "zp", 2)
-        quantize(("far", 2, 1))
-        weave_z(("zn", 2), "V", 0, 4)
-        lag_pass(0, 0, "zp", 2)
-        lag_pass(0, 1, "zn", 0)
-        lag_pass(1, 1, "zn", 0)
-        quantize(("zn", 1))
-        lag_pass(1, 0, "zp", 2)
-        quantize(("zn", 2))
-        lag_pass(0, 0, "zn", 1)
-        lag_pass(1, 0, "zn", 1)
-        weave(("load", 0), "V", 0, 512)
-        weave(("load", 1), "V", 0, 192)
-        quantize(("load", 0))
-        quantize(("load", 1))
-        lag_pass(0, 0, "zn", 2)
-        weave(("far", 0, 2), "V", 0, 512)
+        lag_span(0, "z_now", 1)
+        lag_span(1, "z_now", 1)
+        quantize(("z_prev", 2))
+        lag_span(0, "z_prev", 2)
+        share(("z_now", 2), 4)
+
+        load_far(0, 2, 3)
         load_x(0)
-        lag_pass(0, 1, "zn", 1)
-        lag_pass(0, 1, "zn", 2)
-        lag_out(0, 0)
-        lag_out(0, 1)
-        weave(("lag", 0), "S", 320, 512)
-        lag_pass(1, 0, "zn", 2)
-        lag_pass(2, 0, "zn", 0)
-        lag_pass(1, 1, "zn", 1)
-        lag_pass(1, 1, "zn", 2)
-        lag_pass(1, 1, "zp", 2)
-        weave(("lag", 0), "V", 0, 320)
-        lag_out(1, 0)
-        lag_out(1, 1)
-        quantize(("far", 0, 2))
-        quantize(("lag", 0))
+        load_far(1, 2, 3)
         load_far(2, 2, 3)
-        lag_pass(2, 0, "zn", 1)
-        weave(("far", 1, 2), "V", 0, 320)
+        load_x(1)
+        load_x(2)
+
+        quantize(("far", 2, 1))
+        quantize(("z_now", 2))
+        lag_pass(1, 0, "z_prev", 2)
+
+        interleave(("load", 1), "scalar", 3, 8)
+        interleave(("load", 0), "vector", 0, 8)
+        interleave(("load", 1), "vector", 0, 3)
+        lag_span(0, "z_now", 2)
+        lag_pass(1, 1, "z_prev", 2)
+        lag_span(1, "z_now", 2)
+        lag_out(0)
+        quantize(("load", 0))
+        interleave(("far", 0, 2), "vector", 0, 8)
+        quantize(("load", 1))
+        share(("lag", 0), 5)
+        lag_out(1)
+        lag_pass(2, 0, "z_now", 0)
+        lag_pass(2, 0, "z_now", 1)
+        lag_pass(2, 1, "z_now", 0)
+        quantize(("lag", 0))
+
         comp(0, 0)
+        quantize(("far", 0, 2))
+        interleave(("far", 1, 2), "gpsimd", 1, 8)
         y_out(0, 0)
-        lag_pass(2, 0, "zp", 0)
+        lag_pass(2, 0, "z_prev", 0)
         comp(0, 1)
         y_out(0, 1)
         comp(0, 2)
+        lag_pass(2, 0, "z_now", 2)
         y_out(0, 2)
-        weave(("far", 1, 2), "S", 320, 512)
-        lag_pass(2, 1, "zp", 0)
-        lag_pass(2, 1, "zn", 0)
         comp(0, 3)
-        lag_pass(2, 1, "zn", 1)
-        quantize(("far", 1, 2))
-        load_x(1)
-        lag_pass(2, 0, "zn", 2)
-        weave(("lag", 1), "S", 0, 512)
+        interleave(("far", 1, 2), "scalar", 0, 1)
+        interleave(("lag", 1), "scalar", 0, 8)
+        lag_pass(2, 1, "z_prev", 0)
+        lag_pass(2, 1, "z_now", 1)
+        lag_pass(2, 1, "z_now", 2)
         quantize(("lag", 1))
-        y_out(0, 3)
-        lag_pass(2, 0, "zp", 1)
         comp(1, 0)
-        y_out(1, 0)
-        lag_pass(2, 1, "zn", 2)
-        weave(("far", 2, 2), "S", 0, 512)
-        quantize(("far", 2, 2))
+        y_out(0, 3)
         comp(1, 1)
+        quantize(("far", 1, 2))
+        lag_pass(2, 1, "z_prev", 1)
+        interleave(("far", 2, 2), "scalar", 0, 8)
+        quantize(("far", 2, 2))
+
+        interleave(("y", 0, 0), "gpsimd", 0, 8)
+        interleave(("y", 0, 1), "scalar", 0, 8)
+        lag_pass(2, 0, "z_prev", 1)
+        lag_pass(2, 0, "z_prev", 2)
+        y_out(1, 0)
         comp(1, 2)
-        weave(("y", 0, 0), "S", 64, 512)
+        lag_pass(2, 1, "z_prev", 2)
         y_out(1, 1)
-        lag_pass(2, 0, "zp", 2)
-        weave(("y", 0, 0), "V", 0, 64)
-        lag_pass(2, 1, "zp", 1)
-        lag_pass(2, 1, "zp", 2)
-        lag_out(2, 0)
         comp(1, 3)
         y_out(1, 2)
         y_out(1, 3)
-        load_x(2)
-        lag_out(2, 1)
-        weave(("lag", 2), "V", 0, 512)
-        y_store(0, 0, 2)
-        y_store(0, 2, 4)
-        y_store(1, 0, 2)
-        y_store(1, 2, 4)
-        weave(("y", 0, 1), "S", 0, 512)
-        weave(("y", 1, 0), "S", 128, 512)
-        weave(("y", 1, 1), "S", 0, 512)
+        lag_out(2)
+        share(("lag", 2), 4)
         y_quantize(0, 0)
         quantize(("lag", 2))
+
         comp(2, 0)
         comp(2, 1)
-        comp(2, 2)
+        interleave(("y", 1, 0), "scalar", 0, 8)
         y_quantize(0, 1)
-        words_store(0, 0, 1024)
-        scales_store(0)
-        weave(("y", 1, 0), "V", 0, 128)
+        interleave(("y", 1, 1), "gpsimd", 0, 8)
         y_out(2, 0)
-        comp(2, 3)
+        comp(2, 2)
         y_out(2, 1)
-        y_store(2, 0, 1)
-        y_store(2, 1, 2)
+        comp(2, 3)
         y_out(2, 2)
-        y_store(2, 2, 3)
+        y_out(2, 3)
+        interleave(("y", 2, 0), "scalar", 0, 8)
         y_quantize(1, 0)
         y_quantize(1, 1)
-        weave(("y", 2, 0), "S", 0, 512)
-        scales_store(1)
-        words_store(1, 0, 1024)
-        y_out(2, 3)
-        weave(("y", 2, 1), "V", 0, 512)
         y_quantize(2, 0)
-        y_store(2, 3, 4)
+        share(("y", 2, 1), 5)
         y_quantize(2, 1)
-        words_store(2, 0, 512)
-        words_store(2, 512, 1024)
-        scales_store(2)
+
+        for g in range(LAST):
+            store_y_rows(g, 0, 2)
+            store_y_rows(g, 2, PACK)
+        store_words(0, 0, HALVES)
+        store_scales(0)
+        for h in range(HALVES):
+            store_y_half_rows(LAST, h, 0, 2)
+            store_y_half_rows(LAST, h, 2, PACK)
+        store_scales(1)
+        store_words(1, 0, HALVES)
+        for h in range(HALVES):
+            store_words(LAST, h, h + 1)
+        store_scales(LAST)

from contextlib import ExitStack

import concourse.mybir as mybir
from concourse.masks import make_identity

REGIONS, INDICATORS, COMPOSITES = 1536, 512, 1024
FLOPS = 2 * (2 * REGIONS * REGIONS * INDICATORS + REGIONS * INDICATORS * COMPOSITES)

P = 128
PACK = 4
SPAN = P * PACK
SPANS = REGIONS // SPAN
HALVES = COMPOSITES // SPAN
EIGHTH = SPAN // 8
LAST = SPANS - 1

F32 = mybir.dt.float32
BF16 = mybir.dt.bfloat16
I32 = mybir.dt.int32
U32 = mybir.dt.uint32
U8 = mybir.dt.uint8
FP8X4 = mybir.dt.float8_e4m3fn_x4
FP4X4 = mybir.dt.float4_e2m1fn_x4
MULT = mybir.AluOpType.mult
ADD = mybir.AluOpType.add
COPY = mybir.ActivationFunctionType.Copy

STAGING = (
    (("z_prev", 0), ("far", 1, 1), ("load", 1), ("y", 0, 1), ("y", 1, 1)),
    (("far", 0, 0), ("z_now", 1), ("load", 0), ("lag", 2)),
    (("far", 0, 1), ("far", 2, 0), ("far", 0, 2), ("far", 1, 2), ("y", 2, 1)),
    (("z_now", 0), ("far", 2, 1), ("lag", 0), ("y", 1, 0)),
    (("z_prev", 1), ("z_prev", 2), ("lag", 1), ("y", 2, 0)),
    (("far", 1, 0), ("z_now", 2), ("far", 2, 2), ("y", 0, 0)),
)

LAG_PAIRS = ((0, 1), (2, 3), (0, 1))
Y_PAIRS = ((2, 3, 2, 3), (2, 3, 2, 3), (0, 1, 2, 3))


def tile_local_bivariate_moran_k6_kernel(
    tc, far, z_prev, near_words, near_scales, z_now, gain, load, x, region_weight, out_0, out_1, out_2
):
    nc = tc.nc
    with ExitStack() as ctx:
        sbuf = ctx.enter_context(tc.tile_pool(name="sbuf", bufs=1))
        psum = ctx.enter_context(tc.psum_pool(name="psum", bufs=1))
        ctx.enter_context(tc.manual_schedule())

        rows = {}
        staged = {}
        words, scales = {}, {}
        z_tiles, near, x_tiles, y_tiles, y_words, y_scales = {}, {}, {}, {}, {}, {}
        lag_banks, lag_passes, y_banks = {}, {}, {}

        def bank(pair, n, shape, dtype):
            return psum.tile(shape, dtype, name="bank%d" % (2 * pair + n))

        def by_word(hbm_rows):
            return hbm_rows.rearrange("(p j) w -> p j w", j=PACK)

        def load_z(name, c):
            if c not in z_tiles:
                z_tiles[c] = sbuf.tile([P, 2, PACK, INDICATORS], BF16, name="z_then_x", bufs=SPANS, align_bytes=64)
            source, place = (z_prev, 0) if name == "z_prev" else (z_now, 1)
            rows[(name, c)] = z_tiles[c][:, place, :, :]
            nc.sync.dma_start(out=rows[(name, c)], in_=by_word(source[c * SPAN : (c + 1) * SPAN, :]))

        def load_far(c, g0, g1):
            tile = sbuf.tile([P, PACK, (g1 - g0) * SPAN], BF16, name="far%d_%d" % (c, g0), align_bytes=64)
            nc.sync.dma_start(out=tile[:], in_=by_word(far[c * SPAN : (c + 1) * SPAN, g0 * SPAN : g1 * SPAN]))
            for g in range(g0, g1):
                rows[("far", c, g)] = tile[:, :, (g - g0) * SPAN : (g - g0 + 1) * SPAN]

        def load_near(c):
            near[c] = sbuf.tile([P, 2 * REGIONS], U8, name="near%d" % c, align_bytes=64)
            nc.sync.dma_start(out=near[c][:].bitcast(I32), in_=near_words[c].bitcast(I32))

        def load_near_scales():
            for r in range(4):
                nc.sync.dma_start(
                    out=near_plane[r:P:32, :, :].bitcast(I32),
                    in_=near_scales[:, r:16:4, :].rearrange("c q n -> q c n").bitcast(I32),
                )

        def load_load():
            tile = sbuf.tile([P, PACK, COMPOSITES], BF16, name="load", align_bytes=64)
            nc.sync.dma_start(out=tile[:], in_=by_word(load))
            for h in range(HALVES):
                rows[("load", h)] = tile[:, :, h * SPAN : (h + 1) * SPAN]

        def load_x(g):
            x_tiles[g] = sbuf.tile([P, PACK, COMPOSITES], BF16, name="z_then_x", bufs=SPANS, align_bytes=64)
            nc.sync.dma_start(out=x_tiles[g][:], in_=by_word(x[g * SPAN : (g + 1) * SPAN, :]))

        def interleave(key, engine, lo, hi):
            if key not in staged:
                buffer = [n for n, keys in enumerate(STAGING) if key in keys][0]
                staged[key] = sbuf.tile([P, SPAN, PACK], BF16, name="staged%d" % buffer, align_bytes=64)
            cols = slice(lo * EIGHTH, hi * EIGHTH)
            if engine == "gpsimd":
                src = rows[key][:, :, cols].rearrange("p j w -> p w j")
                nc.gpsimd.tensor_scalar(
                    out=staged[key][:, cols, :], in0=src, scalar1=1.0, scalar2=-0.0, op0=MULT, op1=ADD
                )
                return
            if key[0] in ("z_prev", "z_now"):
                ts = slice(lo // 2, hi // 2)
                dst = staged[key][:].rearrange("p (t a b) j -> p a t b j", t=PACK, b=2)[:, :, ts, :, :]
                src = rows[key].rearrange("p j (a b t) -> p a t b j", t=PACK, b=2)[:, :, ts, :, :]
            else:
                dst = staged[key][:, cols, :].rearrange("p (a i) j -> p a j i", i=4)
                src = rows[key][:, :, cols].rearrange("p j (a i) -> p a j i", i=4)
            copy = nc.vector.tensor_copy if engine == "vector" else nc.scalar.copy
            copy(out=dst, in_=src)

        def share(key, cut):
            interleave(key, "scalar", cut, 8)
            interleave(key, "vector", 0, cut)

        def quantize(key):
            name = "_".join(str(part) for part in key)
            words[key] = sbuf.tile([P, SPAN], U32, name=name + "_words", align_bytes=64)
            scales[key] = sbuf.tile([P, SPAN], U8, name=name + "_scales", align_bytes=64)
            nc.vector.quantize_mx(
                out=words[key][:].bitcast(FP8X4),
                scales=scales[key][:],
                in_=staged[key][:].rearrange("p w j -> p (w j)"),
            )

        def lag_pass(g, b, name, c):
            lag_passes[(g, b)] = lag_passes.get((g, b), 0) + 1
            first, last = lag_passes[(g, b)] == 1, lag_passes[(g, b)] == 2 * SPANS
            if name == "z_prev":
                moving = words[("far", c, g)][:].bitcast(FP8X4)
                moving_scale = scales[("far", c, g)][:]
            else:
                moving = near[c][:, 2 * g * SPAN : 2 * (g + 1) * SPAN].bitcast(FP4X4)
                moving_scale = near_plane[:, c, g * SPAN : (g + 1) * SPAN]
            for n in range(2):
                t = 2 * b + n
                if first:
                    lag_banks[(g, t)] = bank(LAG_PAIRS[g][b], n, [P, SPAN], F32)
                cols = slice(t * P, (t + 1) * P)
                nc.tensor.matmul_mx(
                    out=lag_banks[(g, t)][:],
                    lhsT=words[(name, c)][:, cols].bitcast(FP8X4),
                    lhsT_scale=scales[(name, c)][:, cols],
                    rhs=moving,
                    rhs_scale=moving_scale,
                    start=first,
                    stop=last,
                )

        def lag_span(g, name, c):
            for b in range(2):
                lag_pass(g, b, name, c)

        def lag_out(g):
            rows[("lag", g)] = sbuf.tile([P, PACK, SPAN], BF16, name="lag", bufs=2, align_bytes=64)
            for t in range(PACK):
                nc.scalar.activation(
                    out=rows[("lag", g)][:, t, :].rearrange("p (s m) -> p s m", s=PACK),
                    in_=lag_banks[(g, t)][:].rearrange("p (m s) -> p s m", s=PACK),
                    func=COPY,
                    scale=factors[:, t, SPANS : SPANS + 1],
                )

        def quarter(g, u):
            if g < LAST:
                return [(u, 0), (u, 1)]
            return [(2 * (u % 2), u // 2), (2 * (u % 2) + 1, u // 2)]

        def comp(g, u):
            for n, (s, h) in enumerate(quarter(g, u)):
                cols = slice(s * P, (s + 1) * P)
                y_banks[(g, s, h)] = bank(Y_PAIRS[g][u], n, [P, SPAN], F32)
                nc.tensor.matmul_mx(
                    out=y_banks[(g, s, h)][:],
                    lhsT=words[("lag", g)][:, cols].bitcast(FP8X4),
                    lhsT_scale=scales[("lag", g)][:, cols],
                    rhs=words[("load", h)][:].bitcast(FP8X4),
                    rhs_scale=scales[("load", h)][:],
                    start=True,
                    stop=True,
                )

        def y_out(g, u):
            if u == 0 and g < LAST:
                y_tiles[g] = sbuf.tile([P, PACK, COMPOSITES], F32, name="y%d" % g, align_bytes=64)
                for h in range(HALVES):
                    rows[("y", g, h)] = y_tiles[g][:, :, h * SPAN : (h + 1) * SPAN]
            if u == 0 and g == LAST:
                for h in range(HALVES):
                    rows[("y", g, h)] = sbuf.tile([P, PACK, SPAN], F32, name="y%d_%d" % (g, h), align_bytes=64)
            for s, h in quarter(g, u):
                nc.vector.scalar_tensor_tensor(
                    out=rows[("y", g, h)][:, s, :],
                    in0=y_banks[(g, s, h)][:],
                    scalar=factors[:, s, g : g + 1],
                    in1=x_tiles[g][:, s, h * SPAN : (h + 1) * SPAN],
                    op0=MULT,
                    op1=MULT,
                )

        def plane_row(g):
            return 4 * (g + 1)

        def y_quantize(g, h):
            if h == 0:
                y_words[g] = sbuf.tile([P, COMPOSITES], U32, name="y_words%d" % g, align_bytes=64)
                y_scales[g] = sbuf.tile([P, COMPOSITES], U8, name="y_scales%d" % g, align_bytes=64)
            cols = slice(h * SPAN, (h + 1) * SPAN)
            nc.vector.quantize_mx(
                out=y_words[g][:, cols].bitcast(FP8X4),
                scales=y_scales[g][plane_row(g) : P, cols],
                in_=staged[("y", g, h)][:].rearrange("p w j -> p (w j)"),
            )

        def store_y_rows(g, s0, s1):
            hbm = by_word(out_0[g * SPAN : (g + 1) * SPAN, :])
            nc.sync.dma_start(out=hbm[:, s0:s1, :], in_=y_tiles[g][:, s0:s1, :])

        def store_y_half_rows(g, h, s0, s1):
            hbm = by_word(out_0[g * SPAN : (g + 1) * SPAN, :])
            nc.sync.dma_start(out=hbm[:, s0:s1, h * SPAN : (h + 1) * SPAN], in_=rows[("y", g, h)][:, s0:s1, :])

        def store_words(g, h0, h1):
            hbm = out_1[g].rearrange("p m j -> p (m j)")[:, h0 * SPAN * PACK : h1 * SPAN * PACK]
            nc.sync.dma_start(out=hbm.bitcast(I32), in_=y_words[g][:, h0 * SPAN : h1 * SPAN].bitcast(I32))

        def store_scales(g):
            for r in range(4):
                nc.sync.dma_start(
                    out=out_2[g, r:16:4, :].bitcast(I32), in_=y_scales[g][plane_row(g) + r : P : 32, :].bitcast(I32)
                )

        vectors = sbuf.tile([P, SPAN], BF16, name="vectors", align_bytes=64)
        identity = sbuf.tile([P, P], BF16, name="identity", align_bytes=64)
        factors = sbuf.tile([P, PACK, SPANS + 1], F32, name="factors")
        near_plane = sbuf.tile([P, SPANS, REGIONS], U8, name="near_plane", align_bytes=64)
        make_identity(nc, identity[:])
        nc.vector.memset(vectors[:].bitcast(I32), 0)
        nc.vector.memset(near_plane[:].rearrange("p c n -> p (c n)").bitcast(I32), 0)

        def load_vectors():
            weight_rows = region_weight.rearrange("(g n) -> g n", g=SPANS)
            nc.sync.dma_start(out=vectors[0:LAST, :], in_=weight_rows[0:LAST, :])
            nc.sync.dma_start(out=vectors[LAST:SPANS, :], in_=weight_rows[LAST:SPANS, :])
            nc.sync.dma_start(out=vectors[SPANS : SPANS + 1, :], in_=gain.rearrange("(o n) -> o n", o=1))

        def turn_vectors():
            turned = bank(LAG_PAIRS[1][1], 1, [P, PACK, P], BF16)
            for s in range(PACK):
                nc.tensor.transpose(turned[:, s, :], vectors[:, s:SPAN:PACK], identity[:])
            nc.scalar.activation(out=factors[:], in_=turned[:, :, 0 : SPANS + 1], func=COPY)

        load_z("z_prev", 0)
        load_vectors()
        load_far(0, 0, 2)
        load_z("z_now", 0)
        load_z("z_prev", 1)
        load_far(1, 0, 2)
        load_near(0)
        load_near_scales()
        load_z("z_now", 1)
        load_far(2, 0, 2)
        load_z("z_prev", 2)
        load_near(1)
        load_z("z_now", 2)
        load_load()
        load_near(2)

        share(("z_prev", 0), 4)
        turn_vectors()
        quantize(("z_prev", 0))
        share(("far", 0, 0), 4)
        share(("far", 0, 1), 4)
        quantize(("far", 0, 0))
        share(("z_now", 0), 4)
        quantize(("far", 0, 1))
        lag_span(0, "z_prev", 0)
        lag_span(1, "z_prev", 0)
        share(("z_prev", 1), 4)
        quantize(("z_now", 0))
        share(("far", 1, 0), 4)
        quantize(("z_prev", 1))
        share(("far", 1, 1), 4)
        quantize(("far", 1, 0))
        lag_span(0, "z_prev", 1)
        lag_span(0, "z_now", 0)
        lag_span(1, "z_now", 0)
        share(("z_now", 1), 4)
        quantize(("far", 1, 1))
        lag_span(1, "z_prev", 1)
        quantize(("z_now", 1))

        share(("far", 2, 0), 2)
        interleave(("far", 2, 1), "vector", 0, 6)
        share(("z_prev", 2), 6)
        interleave(("far", 2, 1), "scalar", 6, 8)
        quantize(("far", 2, 0))
        lag_span(0, "z_now", 1)
        lag_span(1, "z_now", 1)
        quantize(("z_prev", 2))
        lag_span(0, "z_prev", 2)
        share(("z_now", 2), 4)

        load_far(0, 2, 3)
        load_x(0)
        load_far(1, 2, 3)
        load_far(2, 2, 3)
        load_x(1)
        load_x(2)

        quantize(("far", 2, 1))
        quantize(("z_now", 2))
        lag_pass(1, 0, "z_prev", 2)

        interleave(("load", 1), "scalar", 3, 8)
        interleave(("load", 0), "vector", 0, 8)
        interleave(("load", 1), "vector", 0, 3)
        lag_span(0, "z_now", 2)
        lag_pass(1, 1, "z_prev", 2)
        lag_span(1, "z_now", 2)
        lag_out(0)
        quantize(("load", 0))
        interleave(("far", 0, 2), "vector", 0, 8)
        quantize(("load", 1))
        share(("lag", 0), 5)
        lag_out(1)
        lag_pass(2, 0, "z_now", 0)
        lag_pass(2, 0, "z_now", 1)
        lag_pass(2, 1, "z_now", 0)
        quantize(("lag", 0))

        comp(0, 0)
        quantize(("far", 0, 2))
        interleave(("far", 1, 2), "gpsimd", 1, 8)
        y_out(0, 0)
        lag_pass(2, 0, "z_prev", 0)
        comp(0, 1)
        y_out(0, 1)
        comp(0, 2)
        lag_pass(2, 0, "z_now", 2)
        y_out(0, 2)
        comp(0, 3)
        interleave(("far", 1, 2), "scalar", 0, 1)
        interleave(("lag", 1), "scalar", 0, 8)
        lag_pass(2, 1, "z_prev", 0)
        lag_pass(2, 1, "z_now", 1)
        lag_pass(2, 1, "z_now", 2)
        quantize(("lag", 1))
        comp(1, 0)
        y_out(0, 3)
        comp(1, 1)
        quantize(("far", 1, 2))
        lag_pass(2, 1, "z_prev", 1)
        interleave(("far", 2, 2), "scalar", 0, 8)
        quantize(("far", 2, 2))

        interleave(("y", 0, 0), "gpsimd", 0, 8)
        interleave(("y", 0, 1), "scalar", 0, 8)
        lag_pass(2, 0, "z_prev", 1)
        lag_pass(2, 0, "z_prev", 2)
        y_out(1, 0)
        comp(1, 2)
        lag_pass(2, 1, "z_prev", 2)
        y_out(1, 1)
        comp(1, 3)
        y_out(1, 2)
        y_out(1, 3)
        lag_out(2)
        share(("lag", 2), 4)
        y_quantize(0, 0)
        quantize(("lag", 2))

        comp(2, 0)
        comp(2, 1)
        interleave(("y", 1, 0), "scalar", 0, 8)
        y_quantize(0, 1)
        interleave(("y", 1, 1), "gpsimd", 0, 8)
        y_out(2, 0)
        comp(2, 2)
        y_out(2, 1)
        comp(2, 3)
        y_out(2, 2)
        y_out(2, 3)
        interleave(("y", 2, 0), "scalar", 0, 8)
        y_quantize(1, 0)
        y_quantize(1, 1)
        y_quantize(2, 0)
        share(("y", 2, 1), 5)
        y_quantize(2, 1)

        for g in range(LAST):
            store_y_rows(g, 0, 2)
            store_y_rows(g, 2, PACK)
        store_words(0, 0, HALVES)
        store_scales(0)
        for h in range(HALVES):
            store_y_half_rows(LAST, h, 0, 2)
            store_y_half_rows(LAST, h, 2, PACK)
        store_scales(1)
        store_words(1, 0, HALVES)
        for h in range(HALVES):
            store_words(LAST, h, h + 1)
        store_scales(LAST)
